import numpy as np, ml_dtypes
CORES = [24,25,26,27,28,29,30,31]
N = 8
import mx_ref
BF = ml_dtypes.bfloat16
def entries(a):
    return np.ascontiguousarray(a.T).reshape(-1)
def table(e):
    return np.ascontiguousarray(np.reshape(e, (-1, 16)).T).astype(np.int32)
def pick(q, e):
    c = np.concatenate([q[0].reshape(128, -1, 4), np.zeros((128, 1, 4), np.uint8)], axis=1); s = np.concatenate([q[1], np.ones((16, 1), np.uint8)], axis=1)
    return (np.ascontiguousarray(c[:, e].reshape(128, -1)), np.ascontiguousarray(s[:, e]))
def join(*qs):
    return (np.concatenate([q[0] for q in qs], axis=1), np.concatenate([q[1] for q in qs], axis=1))
def put(q, e, v):
    c, s = q[0].reshape(128, -1, 4).copy(), q[1].copy(); c[:, e] = v[0].reshape(128, -1, 4); s[:, e] = v[1]
    return (c.reshape(128, -1), s)
def pk(c, s):
    return (np.ascontiguousarray(c), mx_ref.live(s))
def emit(q):
    return q[0], q[1]
def packed(v, rng):
    q = [mx_ref.quantize(np.ascontiguousarray(v[r])) for r in range(N)]
    return np.stack([a for a, b in q]), np.stack([mx_ref.plane(b, rng) for a, b in q])
def f(rng, *shape):
    return mx_ref.flush((rng.standard_normal(shape, dtype=np.float32) * np.exp2(rng.integers(-2, 3, shape[:-1] + (1,)))).astype(BF))
def wide(rng, *shape, cols=0):
    v = rng.standard_normal(shape, dtype=np.float32) * np.exp2(rng.integers(-12, 13, shape)).astype(np.float32)
    if cols: v *= np.repeat(np.exp2(rng.integers(-cols, cols + 1, shape[:-2] + (1, shape[-1] // 4))) * (rng.random(shape[:-2] + (1, shape[-1] // 4)) > 0.0625), 4, axis=-1).astype(np.float32)
    return mx_ref.flush(v.astype(BF))
C, CB, CAPP, S = 512, 128, 80, 512
def counts(rng, total, cap, least):
    n = np.array(least)
    while n.sum() < total: n[rng.choice(np.flatnonzero(n < cap))] += 1
    return n
def runs(rng, least, cap):
    n = np.zeros((N, N), int)
    for s in range(N)[::-1]: n[s] = counts(rng, C, np.minimum(cap[s], CAPP + n[N - 1]), least[s])
    return n
def keeps(rng, n, fall=0, least=np.zeros((N, N), int)):
    k = np.zeros((N, N), int)
    for s in range(N)[::-1]:
        above = k.sum(axis=0)
        k[s] = np.clip(np.minimum(rng.integers(0, 2 * n[s] // 3 + 1), n[s] - fall), np.maximum(n[s] - above, least[s]), np.minimum(np.minimum(n[s], CAPP), S - above))
    return k
def lists(rng, n, k, ends=False, narrow=False):
    p = np.sort(rng.choice(65536 - 2 * N * S, N - 1, replace=False)) + 2 * S * np.arange(1, N)
    if ends: p[0] = int(k[:, 0].sum()) + 2 + int(rng.integers(0, 4))
    if narrow: p[-1] = 65535
    lo, hi = np.append(0, p), np.append(p, 65536)
    keys = [[] for s in range(N)]
    for d in range(N):
        e, i, j = int(ends), -1, -1
        u = lo[d] + e + rng.choice(int(hi[d] - lo[d]) - 2 * e, int(k[:, d].sum()), replace=False)
        at = np.append(np.cumsum(k[::-1, d])[::-1], 0)[1:]
        if ends:
            low, c = np.flatnonzero(n[:, d] - k[:, d] > 1), np.flatnonzero(k[:, d] > 1)
            c = c[c > low[0]]
            if d in (0, N - 1): c = c[c < N - 1]
            i = rng.choice(c); j = rng.choice(low[low < i])
            u[at[i]] = lo[d]; u[at[i] + 1] = hi[d] - 1
        for s in range(N):
            m = at[i] + np.arange(2) if s == j else np.zeros(0, int)
            old = np.concatenate([m, rng.permutation(np.setdiff1d(np.arange(at[s]), m))])[:n[s, d] - k[s, d]]
            keys[s].append(u[np.concatenate([old, at[s] + np.arange(k[s, d])])])
    return {"ky": np.stack([table(np.sort(np.concatenate(v))) for v in keys]), "sp": np.stack([table(np.append(p, np.full(17 - N, 65535)))] * N)}
def setup_inputs(rng):
    kc, ks = packed(f(rng, N, 128, 4 * C), rng)
    n = runs(rng, rng.integers(1, CAPP // 2 + 1, (N, N)), np.full((N, N), CB))
    return {"kc": kc, "ks": ks, "w": f(rng, N, 128, 512), **lists(rng, n, keeps(rng, n))}
def setup_inputs_single(rng):
    least, cap = rng.integers(1, CAPP // 2 + 1, (N, N)), np.full((N, N), CB)
    least[:, N - 1] = rng.integers(0, 2, N); least[rng.permutation(N - 1)[:2], N - 1] = 1; cap[:, N - 1] = least[:, N - 1]
    n = runs(rng, least, cap)
    return {**setup_inputs(rng), **lists(rng, n, keeps(rng, n), narrow=True)}
def setup_inputs_narrow(rng):
    least, cap = rng.integers(1, CAPP // 2 + 1, (N, N)), np.full((N, N), CB)
    least[:, N - 1] = 0; cap[:, N - 1] = 0
    n = runs(rng, least, cap)
    return {**setup_inputs(rng), **lists(rng, n, keeps(rng, n), narrow=True)}
def setup_inputs_full(rng):
    h = int(rng.integers(0, N)); least = np.ones((N, N), int)
    a = np.append(h, rng.permutation(np.delete(np.arange(N), h)))[:(C - N) // CAPP]
    least[N - 1, a] = CAPP
    for s in range(N - 1): least[s, np.append(h, rng.permutation(a[1:]))[:(C - N) // CB]] = CB
    n = runs(rng, least, np.full((N, N), CB)); k = keeps(rng, n)
    v = np.zeros(N, int); v[N - 2:] = CAPP; v[rng.permutation(N - 2)[:S // CAPP - 2]] = CAPP
    k[:, h] = counts(rng, S, CAPP, v)
    return {**setup_inputs(rng), **lists(rng, n, k)}
def setup_inputs_edges(rng):
    q = int(rng.integers(1, N)); h = int(rng.choice(np.delete(np.arange(N - 1), min(q, N - 2))))
    least, cap = rng.integers(2, CAPP // 2 + 1, (N, N)), np.full((N, N), CB)
    least[h, q] = 0; cap[h, q] = 0
    few = rng.integers(2, 5, N)
    few[rng.permutation(np.setdiff1d(np.arange(N), [int(rng.integers(0, N - 2)), N - 2]))[:int(rng.integers(2, N - 1))]] = 0
    least[:, 0] = few; cap[:, 0] = few
    n = runs(rng, least, cap)
    two = np.zeros((N, N), int); two[N - 2, [0, N - 1]] = 2
    return {**setup_inputs(rng), **lists(rng, n, keeps(rng, n, 2, two), ends=True)}
def setup_inputs_spread(rng):
    d = setup_inputs(rng); d["kc"], d["ks"] = packed(wide(rng, N, 128, 4 * C, cols=8), rng); return d
def check_inputs(d):
    b = []
    p = entries(d["sp"][0]).astype(np.int64); g = p[:N - 1]
    if (d["sp"] != d["sp"][:1]).any() or (p[N - 1:] != 65535).any() or g.min() < 1 or g.max() > 65535 or (np.diff(g) <= 0).any(): b.append("sp")
    lo, hi = np.append(0, g), np.append(g, 65536)
    k = [entries(d["ky"][s]).astype(np.int64) for s in range(N)]
    bad = any(v.min() < 0 or v.max() > 65535 or (np.diff(v) <= 0).any() for v in k)
    x, s = np.concatenate(k), np.repeat(np.arange(N), C)
    o = np.argsort(x, kind="stable"); o = o[np.append(x[o][1:] != x[o][:-1], True)]
    x, s = x[o], s[o]
    for q in range(N):
        m = (x >= lo[q]) & (x < hi[q])
        if max(((v >= lo[q]) & (v < hi[q])).sum() for v in k) > CB or m.sum() > S or np.bincount(s[m], minlength=N).max() > CAPP: bad = True
    if bad: b.append("ky")
    return b
def reference(kc, ks, w, ky, sp):
    every = join(*[pk(kc[s], ks[s]) for s in range(N)])
    keys = np.concatenate([entries(ky[s]) for s in range(N)])
    oc, osc = np.zeros((N, 128, 4 * S), np.uint8), np.zeros((N, 16, S), np.uint8)
    ok, y = np.zeros((N, 2, S), np.float32), np.zeros((N, 128, S), np.float32)
    for d in range(N):
        p = entries(sp[d])[:N - 1]
        lo, hi = np.append(0, p)[d], np.append(p, 65536)[d]
        e = np.flatnonzero((keys >= lo) & (keys < hi))
        e = e[np.argsort(keys[e], kind="stable")]
        e = e[np.append(keys[e][1:] != keys[e][:-1], True)[:e.size]]
        a = np.full(S, -1); a[:e.size] = e
        kept = pick(every, a)
        oc[d], osc[d] = emit(kept)
        ok[d, 0] = np.where(a >= 0, keys[a], -1); ok[d, 1] = np.where(a >= 0, a // C, -1)
        y[d] = mx_ref.matmul(mx_ref.quantize(np.ascontiguousarray(w[d])), kept)
    return {"oc": oc, "osc": osc, "ok": ok, "y": y}

@@ -1,0 +1,340 @@
+from concourse.bass import DstId, RemoteDMATransfer
+from concourse.mybir import dt, AluOpType, AxisListType, ActivationFunctionType
+
+SCRATCH = {"mykd": ("dram", [128, 8], "int32"), "kd0": ("dram", [4, 128, 8], "int32"), "kd1": ("dram", [4, 128, 8], "int32"),
+           "acc": ("psum", [128, 1024], "float32")}
+SIZES = {
+    (128, "float32"): "tkf:32 blo:32 m0:512 xb:512 xg:256 val:256 vk:256 vc:256 ta0:32 ta1:32 bl0:32 bl1:32 ps:32 it:1024 ix:112 ik:12 ico:96 irk:96 "
+                      "cst:96 jf:6 pd:6 jt:6 one:32 s0:16 wi:1024 wt:768 qk:24 qi:32 xt:32 yy:64 ot:64 kx:24 mm:768 xf:672 x6:16 nx6:16 sm:4 p6:8 "
+                      "p6b:6 kg:96 va2:96 w2:896 w2t:512 t3:48 yf:656 yo:512",
+    (32, "float32"): "itr:16 tr:16 spf:1 spm:32 spb:32 d7:112 d7s:112 rs7:112 d96:20 c4:64 a2:32 fs:16 kb:20 f1:16 nk:16 zz:20 pl:64 pt:64 cc:64 cy:32 "
+                     "pq:16 pf:16 c5:64 a5:32 sr:32 sx:32 sy:64 so:64 c6:128 a6:64 k2:64 ro:64",
+    (128, "bfloat16"): "cm0:512 cm1:512 ct0:512 ct1:512 cs0:512 cs1:512 eq:512 et:512 es:512 rs32:512 rs16:512 zb:512 wb:512 jk:2560 cb0:640 cb1:640",
+    (128, "int32"): "tk:32 ti0:32 ti1:32 pi:8", (32, "int32"): "spi:1",
+    (128, "uint16"): "xu:512 of0:16 of1:16 mo:48 oxn:32 oxg:16 ovk:16 okg:6 ox6:2 pw:16 off:48 pu:6 of2:32",
+    (128, "float8_e4m3fn_x4"): "zc:128 kcs:512 qc:640 lc:656 fc:512 wc:128",
+    (128, "uint8"): "zs:128 kss:512 qs:640 ls:672 fz:512 wz:128"}
+for (_p, _d), _l in SIZES.items():
+    for _x in _l.split():
+        SCRATCH[_x.split(":")[0]] = ("sbuf", [_p, int(_x.split(":")[1])], _d)
+SEMAPHORES = ["vs", "ss", "ts", "gs", "dk", "dt", "dsp", "dw", "dkc", "dz", "dta", "dtb", "dkx", "doc", "doc2", "dos", "dy", "dy2", "dok",
+              "rk", "rx", "rc", "rs", "loc"]
+
+
+def rank_program(g, core, T, topo):
+    s = T.rank_of(core)
+    if s is None:
+        return
+    A, N = AluOpType, len(T.cores)
+    AF = ActivationFunctionType
+    q_of = {"v": g.vector, "s": g.scalar, "t": g.tensor, "g": g, "y": g.sync}
+    own = {"v": "vs", "s": "ss", "t": "ts", "g": "gs"}
+    tot = {n: 0 for n in SEMAPHORES}
+    seen = {q: {} for q in q_of}
+    wr, rd = {}, {}
+
+    def need(q, r, w, add=False):
+        deps = [(d, 0) for t in r for d in wr.get(t, [])]
+        deps += [(d, 1) for t in w for d in wr.get(t, []) + rd.get(t, [])]
+        for (sem, n), order in deps:
+            if order and add and own.get(q) == sem:
+                continue
+            n = tot[sem] if n is None else n
+            if seen[q].get(sem, 0) < n:
+                q_of[q].wait_ge(T.sem[sem], n)
+                seen[q][sem] = n
+
+    def note(me, r, w, add=False):
+        for t in r:
+            rd.setdefault(t, []).append(me)
+        for t in w:
+            wr[t] = wr.get(t, []) + [me] if add else [me]
+            if not add:
+                rd[t] = []
+
+    def E(q, call, r, w, *args, add=False, **kw):
+        need(q, r, w, add)
+        sem = own[q]
+        call(*args, **kw).then_inc(T.sem[sem], 1)
+        tot[sem] += 1
+        note((sem, tot[sem]), r, w, add)
+
+    def D(q, sem, out, in_, r, w, add=True):
+        need(q, r, [] if add == "par" else w)
+        q_of[q].dma_start(out, in_).then_inc(T.sem[sem], 16)
+        tot[sem] += 16
+        note((sem, None), r, w, True)
+
+    V, S = g.vector, g.scalar
+
+    def copy(r, w, out, in_, add=False): E("v", V.tensor_copy, r, w, out, in_, add=add)
+    def tt(r, w, out, a, b, op, add=False): E("v", V.tensor_tensor, r, w, out, a, b, op, add=add)
+    def ts(r, w, out, a, s1, op, s2=None, op1=None, add=False):
+        if op1 is None: E("v", V.tensor_scalar, r, w, out, a, s1, None, op, add=add)
+        else: E("v", V.tensor_scalar, r, w, out, a, s1, s2, op, op1, add=add)
+    def tp(r, w, out, in_, add=False): E("v", V.transpose, r, w, out, in_, add=add)
+    def scan(r, w, out, a, b, init, o0, o1, add=False): E("v", V.tensor_tensor_scan, r, w, out, a, b, init, o0, o1, add=add)
+    def fill(w, ap, c, add=False): E("v", V.memset, [], w, ap, c, add=add)
+    def iota(w, ap, pat, base, mult=0):
+        E("g", g.iota, [], w, ap, pat, base, mult, allow_small_or_imprecise_dtypes=True)
+
+    def fused(pairs, sem, per, r):
+        need("g", r, [])
+        tr = []
+        for i, (c, dst, src) in enumerate(pairs):
+            rid, pid, _ = topo.addr(c)
+            e = topo.engines(core, c)[per * i:per * (i + 1)]
+            tr.append(RemoteDMATransfer(dst_ids=[DstId(rid=rid, pnc=pid)], dma_engine_mask=sum(1 << k for k in e),
+                                        remote_sem=T.sem[sem], src=src, dst=dst))
+        g.remote_dma_fused(tr, local_sem=T.sem.loc)
+        tot["loc"] += per * len(pairs)
+
+    passes = [h for h in (0, 1) if any(2 * a + h > s for a in range(4))]
+    first = {h: min(a for a in range(4) if 2 * a + h > s) for h in passes}
+
+    if s > 0:
+        for k in (0, 1):
+            D("y" if k == 0 else "s", "dk", T.mykd[64 * k:64 * k + 64, :], T.ky[:], [], ["mykd"], "par")
+    for k in range(8):
+        D("y" if k % 2 == 0 else "s", "dt", T.tk[16 * k:16 * k + 16, :], T.ky[:], [], ["tk"], "par")
+    for k in (0, 1):
+        D("y", "dsp", T.spi[16 * k:16 * k + 16, :], T.sp[:], [], ["spi"], "par")
+    D("y", "dkc", T.kcs[:].bitcast(dt.uint8), T.kc[:], [], ["kcs"], "par")
+    D("y", "dkc", T.kss[:], T.ks[:], [], ["kss"], "par")
+    D("y", "dw", T.wb[:], T.w[:], [], ["wb"], "par")
+
+    iota(["pi"], T.pi[:, 0:1], [[0, 1]], 0, 1)
+    iota(["imo"], T.ix[:, 0:48], [[1, 24], [0, 2]], 0)
+    iota(["ixn"], T.ix[:, 48:80], [[64, 8], [16, 2], [32, 2]], 0)
+    iota(["ixg"], T.ix[:, 80:96], [[64, 8], [16, 2]], 0)
+    iota(["ivk"], T.ix[:, 96:112], [[32, 16]], 0)
+    if s > 0:
+        fused([(T.cores[r], T["kd%d" % (s % 2)][s // 2], T.mykd[:]) for r in range(s)], "rk", 2, ["mykd"])
+    iota(["itr"], T.itr[:], [[16, 16]], 768)
+    iota(["vc"], T.vc[:], [[1, 16], [16, 16]], 0)
+    iota(["it"], T.it[:], [[-1, 1024]], -(66000 + 768 * s))
+    iota(["ikg"], T.ik[:, 0:6], [[80, 2], [32, 3]], 0)
+    iota(["ico"], T.ico[:], [[80, 2], [32, 3], [1, 16]], 16)
+    iota(["irk"], T.irk[:], [[1, 2], [0, 48]], 1)
+    iota(["ijt"], T.ik[:, 6:12], [[16, 6]], 768)
+
+    for h in passes:
+        if first[h]:
+            fill(["ti%d" % h], T["ti%d" % h][0:32 * first[h], :], -1)
+    ts(["pi"], ["pi1"], T.pi[:, 1:2], T.pi[:, 0:1], 15, A.bitwise_and)
+    ts(["pi"], ["pi2"], T.pi[:, 2:3], T.pi[:, 0:1], 4, A.logical_shift_right, 1, A.bitwise_and)
+    ts(["pi"], ["pi3"], T.pi[:, 3:4], T.pi[:, 0:1], 5, A.logical_shift_right)
+    fill(["rs32"], T.rs32[:], 1.0)
+    fill(["rs16"], T.rs16[:], 1.0)
+    fill(["rs7"], T.rs7[:], 1.0)
+    copy(["pi1", "pi2", "pi3"], ["ps"], T.ps[:, 0:3], T.pi[:, 1:4])
+    P = lambda k: T.ps[:, k:k + 1]
+    copy(["imo"], ["mo"], T.mo[:], T.ix[:, 0:48])
+    ts(["ps"], ["ps3"], P(3), P(1), 16.0, A.mult, P(0), A.add)
+    ts(["ps"], ["ps4"], P(4), P(1), 32.0, A.mult, P(0), A.add)
+    ts(["ps"], ["ps7"], P(7), P(1), 256.0, A.mult)
+    ts(["ps"], ["ps10"], P(10), P(0), 0.0, A.is_equal)
+    ts(["ps"], ["ps11"], P(11), P(0), 0.0, A.not_equal, -1.0, A.mult)
+    ts(["ps"], ["ps14"], P(14), P(0), 0.0, A.not_equal)
+    ts(["ixn", "ps"], ["oxn"], T.oxn[:], T.ix[:, 48:80], P(0), A.add)
+    ts(["ixg", "ps4"], ["oxg"], T.oxg[:], T.ix[:, 80:96], P(4), A.add)
+    ts(["ivk", "ps3"], ["ovk"], T.ovk[:], T.ix[:, 96:112], P(3), A.add)
+    fill(["one"], T.one[:], 1.0)
+    fill(["kb"], T.kb[:], 1.0)
+    fill(["rs7"], T.rs7[:, 0:112:7], 0.0)
+    fill(["rs32"], T.rs32[:, 0:512:32], 0.0)
+    fill(["rs16"], T.rs16[:, 0:512:16], 0.0)
+    fill(["zz"], T.zz[:], 0.0)
+    fill(["pl"], T.pl[:], 0.0)
+    fill(["cc"], T.cc[:], 0.0)
+    fill(["d96"], T.d96[:], 0.0)
+    fill(["kb"], T.kb[:, 0:1], 0.0)
+    fill(["qi"], T.qi[:], 0.0)
+    copy(["tk"], ["tkf"], T.tkf[:], T.tk[:])
+    tp(["tkf"], ["blo"], T.blo[:], T.tkf[:])
+    copy(["blo", "mo"], ["m0"], T.m0[:], T.blo[:, 0:32].indirect(T.mo[:, 0:32]))
+    tp(["m0"], ["xb"], T.xb[:], T.m0[:])
+    E("s", S.activation, ["xb", "ovk", "ps11"], ["vk"], T.vk[:], T.xb[:, 0:512].indirect(T.ovk[:, 0:16]), AF.Copy, scale=P(11))
+    E("s", S.activation, ["it", "ps14"], ["wi"], T.wi[:], T.it[:], AF.Copy, scale=P(14))
+    if passes:
+        copy(["xb", "oxn"], ["xu"], T.xu[:], T.xb[:, 0:512].indirect(T.oxn[:, 0:32]))
+        copy(["xb", "oxg"], ["xg"], T.xg[:], T.xb[:, 0:512].indirect(T.oxg[:, 0:16]))
+    copy(["spi"], ["spf"], T.spf[:], T.spi[:])
+    ts(["one", "spf"], ["spm"], T.spm[:], T.one[0:32, :], T.spf[:, 0:1], A.mult)
+    tp(["spm"], ["spb"], T.spb[:], T.spm[:])
+    for e in range(N - 1):
+        ts(["blo", "spb"], ["d7"], T.d7[:, e:112:7], T.blo[0:32, 0:16], T.spb[:, e:e + 1], A.is_ge, 96.0, A.mult, add=True)
+    scan(["d7", "rs7"], ["d7s"], T.d7s[:], T.rs7[:], T.d7[:], 0.0, A.mult, A.add)
+    copy(["d7s"], ["d96"], T.d96[:, 0:16], T.d7s[:, 6:112:7])
+    ts(["itr", "ps"], ["tr"], T.tr[:], T.itr[:], T.ps[0:32, 0:1], A.add)
+    ts(["vc", "ps7", "ps10"], ["vc"], T.vc[:], T.vc[:], P(7), A.add, P(10), A.mult)
+    tt(["vk", "vc"], ["val"], T.val[:], T.vk[:], T.vc[:], A.add)
+
+    if passes:
+        tot["rk"] = 2 * (N - 1 - s)
+        wr["rk"] = [("rk", None)]
+        for h in passes:
+            a = first[h]
+            D("y", "dta" if h == 0 else "dtb", T["ti%d" % h][32 * a:128, :], T["kd%d" % h][a:4], ["rk"], ["ti%d" % h], True)
+        H = ["%d" % h for h in passes]
+        for h in H: copy(["ti" + h], ["ta" + h], T["ta" + h][:], T["ti" + h][:])
+        for h in H: tp(["ta" + h], ["bl" + h], T["bl" + h][:], T["ta" + h][:])
+        for h in H: ts(["xu", "bl" + h], ["cm" + h], T["cm" + h][:], T.xu[:], T["bl" + h][:, 0:1], A.is_ge)
+        for h in H: tp(["cm" + h], ["ct" + h], T["ct" + h][:], T["cm" + h][:])
+        for h in H: scan(["ct" + h, "rs32"], ["cs" + h], T["cs" + h][:], T.rs32[:], T["ct" + h][:], 0.0, A.mult, A.add)
+        for h in H: ts(["cs" + h], ["of" + h], T["of" + h][:], T["cs" + h][:, 31:512:32], 1.0, A.subtract, 0.0, A.max)
+        for i, h in enumerate(H):
+            tt(["ta" + h, "of" + h, "xg"], ["eq"], T.eq[:, 256 * i:256 * i + 256], T["ta" + h][:, 0:32].indirect(T["of" + h][:, 0:16]), T.xg[:], A.is_equal, add=True)
+        n = 256 * len(H)
+        tp(["eq"], ["et"], T.et[:, 0:n], T.eq[:, 0:n])
+        scan(["et", "rs16"], ["es"], T.es[:, 0:n], T.rs16[:, 0:n], T.et[:, 0:n], 0.0, A.mult, A.add)
+        if len(H) == 2: tt(["es"], ["s0"], T.s0[:], T.es[:, 15:256:16], T.es[:, 271:512:16], A.add)
+        else: copy(["es"], ["s0"], T.s0[:], T.es[:, 15:256:16])
+        quads = list(range(min(first.values()), 4))
+        for i, a in enumerate(quads):
+            copy(["s0"], ["c4"], T.c4[:, 16 * i:16 * i + 16], T.s0[32 * a:32 * a + 32, :], add=True)
+        if len(quads) == 4:
+            tt(["c4"], ["a2"], T.a2[:], T.c4[:, 0:32], T.c4[:, 32:64], A.add)
+            tt(["a2"], ["fs"], T.fs[:], T.a2[:, 0:16], T.a2[:, 16:32], A.add)
+        elif len(quads) == 3:
+            tt(["c4"], ["a2"], T.a2[:, 0:16], T.c4[:, 0:16], T.c4[:, 16:32], A.add)
+            tt(["a2", "c4"], ["fs"], T.fs[:], T.a2[:, 0:16], T.c4[:, 32:48], A.add)
+        elif len(quads) == 2:
+            tt(["c4"], ["fs"], T.fs[:], T.c4[:, 0:16], T.c4[:, 16:32], A.add)
+        else:
+            copy(["c4"], ["fs"], T.fs[:], T.c4[:, 0:16])
+        ts(["fs"], ["kb"], T.kb[:, 1:17], T.fs[:], 0.0, A.is_equal)
+        ts(["fs"], ["f1"], T.f1[:], T.fs[:], 0.0, A.is_gt)
+    scan(["kb", "zz"], ["pl"], T.pl[:, 0:17], T.kb[:, 0:17], T.zz[:, 0:17], 0.0, A.add, A.add)
+    scan(["kb", "d96"], ["pl"], T.pl[:, 32:49], T.kb[:, 0:17], T.d96[:, 0:17], 0.0, A.add, A.max, add=True)
+    tp(["pl"], ["pt"], T.pt[:], T.pl[:])
+    scan(["pt"], ["cc"], T.cc[:, 1:33], T.pt[:, 0:32], T.pt[:, 32:64], 0.0, A.add, A.max)
+    if passes: tt(["f1", "tr"], ["nk"], T.nk[:], T.f1[:], T.tr[:], A.mult)
+    tp(["cc"], ["cy"], T.cy[:], T.cc[:, 0:32])
+    scan(["kb", "d96", "cy"], ["pq"], T.pq[:], T.kb[:, 0:16], T.d96[:, 0:16], T.cy[:, 16:17], A.add, A.max)
+    src, tok = T.pq, "pq"
+    if passes:
+        tt(["pq", "nk"], ["pf"], T.pf[:], T.pq[:], T.nk[:], A.max)
+        src, tok = T.pf, "pf"
+    for a in range(4):
+        copy([tok], ["pw"], T.pw[32 * a:32 * a + 32, :], src[:], add=True)
+    E("v", V.tensor_copy, ["pw", "val"], ["wi"], T.wi[:, 0:1024].indirect(T.pw[:, 0:16]), T.val[:])
+    tp(["wi"], ["wt"], T.wt[:], T.wi[:, 0:768])
+    tt(["wt"], ["qk"], T.qk[:], T.wt[:, 1:768:32], T.wt[:, 17:768:32], A.max)
+    tt(["wt"], ["qi"], T.qi[:, 0:24], T.wt[:, 0:768:32], T.wt[:, 16:768:32], A.max)
+    peers = [(s + i) % N for i in range(1, N)]
+    fused([(T.cores[d], T.kx[:, 3 * s:3 * s + 3], T.qk[:, 3 * d:3 * d + 3]) for d in peers], "rx", 2, ["qk"])
+    D("y", "dkx", T.kx[:, 3 * s:3 * s + 3], T.qk[:, 3 * s:3 * s + 3], ["qk"], ["kx"], "par")
+    tp(["qi"], ["xt"], T.xt[:], T.qi[:])
+    for k in range(4):
+        copy(["xt"], ["yy"], T.yy[:, 16 * k:16 * k + 16], T.xt[:, 16 * (k // 2):16 * (k // 2) + 16], add=True)
+    tp(["yy"], ["ot"], T.ot[:], T.yy[:])
+    copy(["ot"], ["off"], T.off[:, 0:48:2], T.ot[:, 0:24])
+    copy(["ot"], ["off"], T.off[:, 1:48:2], T.ot[:, 32:56], add=True)
+    def pick(d, cbuf, sbuf, c, tc, tz):
+        E("v", V.tensor_copy, ["off", "kcs"], [tc], cbuf[:, c:c + 80].bitcast(dt.uint32), T.kcs[:, 0:512].bitcast(dt.uint32).indirect(T.off[:, 6 * d:6 * d + 5]))
+        E("s", S.activation, ["off", "kss"], [tz], sbuf[:, c:c + 80], T.kss[:, 0:512].indirect(T.off[:, 6 * d:6 * d + 5]), AF.Copy)
+    for d in peers: pick(d, T.qc, T.qs, 80 * d, "qc%d" % d, "qs%d" % d)
+    pick(s, T.lc, T.ls, 16 + 80 * s, "lco", "lso")
+    me = 16 + 80 * s
+    for part in (peers[:1], peers[1:3], peers[3:]):
+        e = len(topo.engines(core, T.cores[part[0]])) // len(part)
+        fused([(T.cores[d], T.lc[:, me:me + 80].bitcast(dt.uint8), T.qc[:, 80 * d:80 * d + 80].bitcast(dt.uint8)) for d in part], "rc", e, ["qc%d" % d for d in part])
+        fused([(T.cores[d], T.ls[:, me:me + 80], T.qs[:, 80 * d:80 * d + 80]) for d in part], "rs", e, ["qs%d" % d for d in part])
+        for r in part:
+            tot["rc"] += e
+            tot["rs"] += e
+    fill(["zb"], T.zb[:], 0.0)
+    fill(["sr"], T.sr[:], 0.0)
+    fill(["k2"], T.k2[:], 0.0)
+    E("v", V.quantize_mx, ["zb"], ["zc", "zs"], T.zc[:], T.zs[:], T.zb[:])
+    D("y", "dz", T.lc[:, 0:1].bitcast(dt.uint8), T.zc[:, 0:1].bitcast(dt.uint8), ["zc"], ["lcz"], "par")
+    D("y", "dz", T.ls[:, 0:1], T.zs[:, 0:1], ["zs"], ["lsz"], "par")
+    fill(["w2"], T.w2[:], 0.0)
+    fill(["yfz"], T.yf[:, 0:16], 0.0)
+    ts(["ps", "ps3"], ["ps5"], P(5), P(2), 160.0, A.mult, P(3), A.add)
+    ts(["ps"], ["ps6"], P(6), P(1), 16.0, A.mult)
+    ts(["ps"], ["ps8"], P(8), P(2), 2.0, A.mult)
+    ts(["ps"], ["ps9"], P(9), P(2), 6.0, A.mult, P(0), A.add)
+    ts(["ps"], ["ps12"], P(12), P(0), 1.0, A.is_equal)
+    ts(["ps"], ["ps13"], P(13), P(0), 2.0, A.is_equal)
+    ts(["ps", "ps6"], ["ps15"], P(15), P(2), 160.0, A.mult, P(6), A.add)
+    ts(["ps9"], ["ox6"], T.ox6[:, 0:1], P(9), 23.0, A.min)
+    ts(["ikg", "ps5"], ["okg"], T.okg[:], T.ik[:, 0:6], P(5), A.add)
+    ts(["ico", "ps15", "ps10"], ["ico"], T.ico[:], T.ico[:], P(15), A.add, P(10), A.mult)
+    ts(["irk", "ps8", "ps13"], ["irk"], T.irk[:], T.irk[:], P(8), A.add, P(13), A.mult)
+    tt(["ico", "irk"], ["cst"], T.cst[:], T.ico[:], T.irk[:], A.add)
+    ts(["cst", "ps12"], ["cst"], T.cst[:], T.cst[:], P(12), A.subtract)
+    ts(["ijt", "ps"], ["jf"], T.jf[:], T.ik[:, 6:12], P(0), A.add)
+    E("v", V.quantize_mx, ["wb"], ["wc", "wz"], T.wc[:], T.wz[:], T.wb[:])
+    tot["rx"] = 2 * (N - 1)
+    wr["rx"] = [("rx", None)]
+    E("s", S.activation, ["rx", "kx", "mo"], ["mmS"], T.mm[:, 384:768], T.kx[:, 0:24].indirect(T.mo[:, 24:48]), AF.Copy)
+    copy(["rx", "kx", "mo"], ["mmV"], T.mm[:, 0:384], T.kx[:, 0:24].indirect(T.mo[:, 0:24]))
+    copy(["rx", "kx", "ox6"], ["x6"], T.x6[:], T.kx[:, 0:24].indirect(T.ox6[:, 0:1]))
+    ts(["x6"], ["nx6"], T.nx6[:], T.x6[:], -1.0, A.mult)
+    for r in range(N):
+        tp(["mmV" if r < 4 else "mmS"], ["xf3"], T.xf[:, 80 * r + 64:80 * r + 96], T.mm[:, 96 * r + 64:96 * r + 96], add=True)
+    for r in range(N):
+        tp(["mmV" if r < 4 else "mmS", "xf3"], ["xf"], T.xf[:, 80 * r:80 * r + 64], T.mm[:, 96 * r:96 * r + 64], add=True)
+    for e in range(4):
+        E("s", S.activation, ["xf", "xf3", "nx6"], ["jk%d" % e, "sm%d" % e], T.jk[:, 640 * e:640 * e + 640], T.xf[:, 0:640], AF.Sign, bias=T.nx6[:, e:e + 1], accum_out=T.sm[:, e:e + 1])
+    ts(["xf", "xf3", "okg", "ps12"], ["kg"], T.kg[:], T.xf[:, 0:656].indirect(T.okg[:, 0:6]), P(12), A.mult)
+    ts(["xf", "x6"], ["cb0"], T.cb0[:], T.xf[:, 0:640], T.x6[:, 4:5], A.is_gt)
+    ts(["xf", "x6"], ["cb1"], T.cb1[:], T.xf[:, 0:640], T.x6[:, 5:6], A.is_gt)
+    tt(["kg", "cst"], ["va2"], T.va2[:], T.kg[:], T.cst[:], A.add)
+    ts(["x6"], ["pd"], T.pd[:], T.x6[:, 0:6], -65536.0, A.is_lt)
+    for k in (0, 1):
+        E("v", V.tensor_reduce, ["cb%d" % k], ["p6%d" % k], T.p6[:, 4 + k:5 + k], T["cb%d" % k][:], AxisListType.X, A.add)
+    tt(["pd", "jf"], ["jt"], T.jt[:], T.pd[:], T.jf[:], A.mult)
+    ts(["sm%d" % e for e in range(4)], ["p6"], T.p6[:, 0:4], T.sm[:], 639.0, A.add, 0.5, A.mult)
+    tt(["p6", "p60", "p61", "jt"], ["p6b"], T.p6b[:], T.p6[:, 0:6], T.jt[:], A.max)
+    copy(["p6b"], ["pu"], T.pu[:], T.p6b[:])
+    E("v", V.tensor_copy, ["pu", "va2"], ["w2"], T.w2[:, 0:896].indirect(T.pu[:, 0:6]), T.va2[:], add=True)
+    tp(["w2"], ["w2t"], T.w2t[:], T.w2[:, 0:512])
+    tt(["w2t"], ["t3"], T.t3[:, 0:16], T.w2t[:, 0:512:32], T.w2t[:, 16:512:32], A.add)
+    for a in range(4):
+        copy(["t3"], ["c5"], T.c5[:, 16 * a:16 * a + 16], T.t3[32 * a:32 * a + 32, 0:16], add=True)
+    tt(["c5"], ["a5"], T.a5[:], T.c5[:, 0:32], T.c5[:, 32:64], A.add)
+    tt(["a5"], ["sr"], T.sr[:, 0:16], T.a5[:, 0:16], T.a5[:, 16:32], A.add)
+    tp(["sr"], ["sx"], T.sx[:], T.sr[:])
+    for k in range(4):
+        copy(["sx"], ["sy"], T.sy[:, 16 * k:16 * k + 16], T.sx[:, 16 * (k // 2):16 * (k // 2) + 16], add=True)
+    tp(["sy"], ["so"], T.so[:], T.sy[:])
+    for a in range(4):
+        copy(["so"], ["of2"], T.of2[32 * a:32 * a + 32, 0:32:2], T.so[:, 0:16], add=True)
+        copy(["so"], ["of2"], T.of2[32 * a:32 * a + 32, 1:32:2], T.so[:, 32:48], add=True)
+    wr["lca"], wr["lsa"] = [("rc", None)], [("rs", None)]
+    land, lands = ["lca", "lco", "lcz"], ["lsa", "lso", "lsz"]
+    for k in (0, 1):
+        c = 16 + 320 * k
+        E("t", g.tensor.matmul_mx, land + lands + ["wc", "wz"], ["acc%d" % k], T.acc[:, 512 * k:512 * k + 320], T.wc[:], T.wz[:], T.lc[:, c:c + 320], T.ls[:, c:c + 320], True, True)
+    for k in (0, 1):
+        E("s", S.activation, ["acc%d" % k], ["yf%d" % k], T.yf[:, 16 + 320 * k:336 + 320 * k], T.acc[:, 512 * k:512 * k + 320], AF.Copy)
+    ys = ["yfz", "yf0", "yf1", "of2"]
+    def codes(k):
+        E("v", V.tensor_copy, land + ["of2"], ["fc%d" % k], T.fc[:, 256 * k:256 * k + 256].bitcast(dt.uint32), T.lc[:, 0:656].bitcast(dt.uint32).indirect(T.of2[:, 16 * k:16 * k + 16]))
+        D("y", ["doc", "doc2"][k], T.oc[:, 1024 * k:1024 * k + 1024], T.fc[:, 256 * k:256 * k + 256].bitcast(dt.uint8), ["fc%d" % k], ["oc"], "par")
+    codes(0)
+    E("s", S.activation, ys, ["yo0"], T.yo[:, 0:256], T.yf[:, 0:656].indirect(T.of2[:, 0:16]), AF.Copy)
+    D("y", "dy", T.y[:, 0:256], T.yo[:, 0:256], ["yo0"], ["y"], "par")
+    codes(1)
+    E("s", S.activation, lands + ["of2"], ["fz"], T.fz[:], T.ls[:, 0:656].indirect(T.of2[:, 0:32]), AF.Copy)
+    for k in range(4):
+        D("s", "dos", T.osc[4 * k:4 * k + 4, :], T.fz[32 * k:32 * k + 4, :], ["fz"], ["osc"], "par")
+    copy(ys, ["yo1"], T.yo[:, 256:512], T.yf[:, 0:656].indirect(T.of2[:, 16:32]))
+    D("y", "dy2", T.y[:, 256:512], T.yo[:, 256:512], ["yo1"], ["y"], "par")
+    tt(["w2t"], ["t3k"], T.t3[:, 16:32], T.w2t[:, 1:512:32], T.w2t[:, 17:512:32], A.add)
+    tt(["w2t"], ["t3k"], T.t3[:, 32:48], T.w2t[:, 2:512:32], T.w2t[:, 18:512:32], A.add, add=True)
+    for a in range(4):
+        copy(["t3k"], ["c6"], T.c6[:, 32 * a:32 * a + 32], T.t3[32 * a:32 * a + 32, 16:48], add=True)
+    tt(["c6"], ["a6"], T.a6[:], T.c6[:, 0:64], T.c6[:, 64:128], A.add)
+    tt(["a6"], ["c6b"], T.c6[:, 0:32], T.a6[:, 0:32], T.a6[:, 32:64], A.add)
+    ts(["c6b"], ["k2"], T.k2[:, 0:16], T.c6[:, 0:16], -1.0, A.mult, 1.0, A.subtract, add=True)
+    ts(["c6b"], ["k2"], T.k2[:, 32:48], T.c6[:, 16:32], 1.0, A.subtract, add=True)
+    tp(["k2"], ["ro"], T.ro[:], T.k2[:])
+    D("y", "dok", T.ok[0:1, :], T.ro[0:16, 0:32], ["ro"], ["ok"], "par")
+    D("y", "dok", T.ok[1:2, :], T.ro[0:16, 32:64], ["ro"], ["ok"], "par")
+    for n in SEMAPHORES:
+        if tot[n]:
+            g.wait_ge(T.sem[n], tot[n])

@@ -4,12 +4,12 @@ from concourse.mybir import dt, AluOpType, AxisListType, ActivationFunctionType
 SCRATCH = {"mykd": ("dram", [128, 8], "int32"), "kd0": ("dram", [4, 128, 8], "int32"), "kd1": ("dram", [4, 128, 8], "int32"),
            "acc": ("psum", [128, 1024], "float32")}
 SIZES = {
-    (128, "float32"): "tkf:32 blo:32 m0:512 xb:512 xg:256 val:256 vk:256 vc:256 ta0:32 ta1:32 bl0:32 bl1:32 ps:32 it:1024 ix:112 ik:12 ico:96 irk:96 "
-                      "cst:96 jf:6 pd:6 jt:6 one:32 s0:16 wi:1024 wt:768 qk:24 qi:32 xt:32 yy:64 ot:64 kx:24 mm:768 xf:672 x6:16 nx6:16 sm:4 p6:8 "
-                      "p6b:6 kg:96 va2:96 w2:896 w2t:512 t3:48 yf:656 yo:512",
-    (32, "float32"): "itr:16 tr:16 spf:1 spm:32 spb:32 d7:112 d7s:112 rs7:112 d96:20 c4:64 a2:32 fs:16 kb:20 f1:16 nk:16 zz:20 pl:64 pt:64 cc:64 cy:32 "
+    (128, "float32"): "tkf:32 blo:32 m0:512 xb:512 xg:256 val:256 vk:256 vc:256 vd:256 ta0:32 ta1:32 bl0:32 bl1:32 ps:32 it:1040 ix:112 ik:6 ico:192 irk:192 "
+                      "cst:96 jf:6 pd:6 jt:12 s0:16 wi:1040 wt:768 qk:24 qi:32 xt:32 yy:64 ot:64 kx:24 mm:768 xf:672 x6:16 nx6:16 sm:6 "
+                      "pm:6 kg:96 va2:96 w2:976 w2t:512 t3:48 yf:656 yo:512",
+    (32, "float32"): "tr:16 spf:1 spm:32 spb:32 d7:112 d7s:112 rs7:112 d96:20 c4:64 a2:32 kb:20 f1:16 nk:16 zz:20 pl:64 pt:64 cc:64 cy:32 "
                      "pq:16 pf:16 c5:64 a5:32 sr:32 sx:32 sy:64 so:64 c6:128 a6:64 k2:64 ro:64",
-    (128, "bfloat16"): "cm0:512 cm1:512 ct0:512 ct1:512 cs0:512 cs1:512 eq:512 et:512 es:512 rs32:512 rs16:512 zb:512 wb:512 jk:2560 cb0:640 cb1:640",
+    (128, "bfloat16"): "cm0:512 cm1:512 ct0:512 ct1:512 cs0:512 cs1:512 eq:512 et:512 es:512 rs32:512 rs16:512 rs160:640 zb:512 wb:512 jk:2560 cb:1280 cbs:1280",
     (128, "int32"): "tk:32 ti0:32 ti1:32 pi:8", (32, "int32"): "spi:1",
     (128, "uint16"): "xu:512 of0:16 of1:16 mo:48 oxn:32 oxg:16 ovk:16 okg:6 ox6:2 pw:16 off:48 pu:6 of2:32",
     (128, "float8_e4m3fn_x4"): "zc:128 kcs:512 qc:640 lc:656 fc:512 wc:128",
@@ -75,8 +75,15 @@ def rank_program(g, core, T, topo):
     def tp(r, w, out, in_, add=False): E("v", V.transpose, r, w, out, in_, add=add)
     def scan(r, w, out, a, b, init, o0, o1, add=False): E("v", V.tensor_tensor_scan, r, w, out, a, b, init, o0, o1, add=add)
     def fill(w, ap, c, add=False): E("v", V.memset, [], w, ap, c, add=add)
+    def act(r, w, out, in_, fn=AF.Copy, **kw): E("s", S.activation, r, w, out, in_, fn, **kw)
     def iota(w, ap, pat, base, mult=0):
         E("g", g.iota, [], w, ap, pat, base, mult, allow_small_or_imprecise_dtypes=True)
+
+    later = []
+
+    def gap(n=1):
+        for _ in range(min(n, len(later))):
+            later.pop(0)()
 
     def fused(pairs, sem, per, r):
         need("g", r, [])
@@ -110,13 +117,22 @@ def rank_program(g, core, T, topo):
     iota(["ivk"], T.ix[:, 96:112], [[32, 16]], 0)
     if s > 0:
         fused([(T.cores[r], T["kd%d" % (s % 2)][s // 2], T.mykd[:]) for r in range(s)], "rk", 2, ["mykd"])
-    iota(["itr"], T.itr[:], [[16, 16]], 768)
     iota(["vc"], T.vc[:], [[1, 16], [16, 16]], 0)
-    iota(["it"], T.it[:], [[-1, 1024]], -(66000 + 768 * s))
+    iota(["it"], T.it[:], [[-1, 1040]], -(66000 + 768 * s))
+    iota(["d96"], T.d96[:], [[0, 20]], 0)
+    iota(["tr"], T.tr[:], [[16, 16]], 768, 1)
+    if not passes:
+        iota(["kb"], T.kb[:], [[0, 20]], 1)
+    iota(["kb"], T.kb[:, 0:1], [[0, 1]], 0)
+    for n, c in (("zz", 20), ("pl", 64), ("cc", 64), ("qi", 32)):
+        iota([n], T[n][:], [[0, c]], 0)
     iota(["ikg"], T.ik[:, 0:6], [[80, 2], [32, 3]], 0)
-    iota(["ico"], T.ico[:], [[80, 2], [32, 3], [1, 16]], 16)
-    iota(["irk"], T.irk[:], [[1, 2], [0, 48]], 1)
-    iota(["ijt"], T.ik[:, 6:12], [[16, 6]], 768)
+    iota(["ico"], T.ico[:, 0:96], [[80, 2], [32, 3], [1, 16]], 16)
+    iota(["irk"], T.irk[:, 0:96], [[1, 2], [0, 48]], 1)
+    iota(["jf"], T.jf[:, 0:4], [[32, 4]], 10897, 2)
+    iota(["jf2"], T.jf[:, 4:6], [[16, 2]], 10832, 1)
+    for n, c in (("sr", 32), ("k2", 64)):
+        iota([n], T[n][:], [[0, c]], 0)
 
     for h in passes:
         if first[h]:
@@ -125,11 +141,11 @@ def rank_program(g, core, T, topo):
     ts(["pi"], ["pi2"], T.pi[:, 2:3], T.pi[:, 0:1], 4, A.logical_shift_right, 1, A.bitwise_and)
     ts(["pi"], ["pi3"], T.pi[:, 3:4], T.pi[:, 0:1], 5, A.logical_shift_right)
     fill(["rs32"], T.rs32[:], 1.0)
-    fill(["rs16"], T.rs16[:], 1.0)
     fill(["rs7"], T.rs7[:], 1.0)
     copy(["pi1", "pi2", "pi3"], ["ps"], T.ps[:, 0:3], T.pi[:, 1:4])
     P = lambda k: T.ps[:, k:k + 1]
     copy(["imo"], ["mo"], T.mo[:], T.ix[:, 0:48])
+    fill(["rs16"], T.rs16[:], 1.0)
     ts(["ps"], ["ps3"], P(3), P(1), 16.0, A.mult, P(0), A.add)
     ts(["ps"], ["ps4"], P(4), P(1), 32.0, A.mult, P(0), A.add)
     ts(["ps"], ["ps7"], P(7), P(1), 256.0, A.mult)
@@ -139,36 +155,46 @@ def rank_program(g, core, T, topo):
     ts(["ixn", "ps"], ["oxn"], T.oxn[:], T.ix[:, 48:80], P(0), A.add)
     ts(["ixg", "ps4"], ["oxg"], T.oxg[:], T.ix[:, 80:96], P(4), A.add)
     ts(["ivk", "ps3"], ["ovk"], T.ovk[:], T.ix[:, 96:112], P(3), A.add)
-    fill(["one"], T.one[:], 1.0)
-    fill(["kb"], T.kb[:], 1.0)
+    ts(["ps7", "ps10"], ["ps16"], P(16), P(7), P(10), A.mult)
     fill(["rs7"], T.rs7[:, 0:112:7], 0.0)
     fill(["rs32"], T.rs32[:, 0:512:32], 0.0)
     fill(["rs16"], T.rs16[:, 0:512:16], 0.0)
-    fill(["zz"], T.zz[:], 0.0)
-    fill(["pl"], T.pl[:], 0.0)
-    fill(["cc"], T.cc[:], 0.0)
-    fill(["d96"], T.d96[:], 0.0)
-    fill(["kb"], T.kb[:, 0:1], 0.0)
-    fill(["qi"], T.qi[:], 0.0)
     copy(["tk"], ["tkf"], T.tkf[:], T.tk[:])
-    tp(["tkf"], ["blo"], T.blo[:], T.tkf[:])
-    copy(["blo", "mo"], ["m0"], T.m0[:], T.blo[:, 0:32].indirect(T.mo[:, 0:32]))
-    tp(["m0"], ["xb"], T.xb[:], T.m0[:])
-    E("s", S.activation, ["xb", "ovk", "ps11"], ["vk"], T.vk[:], T.xb[:, 0:512].indirect(T.ovk[:, 0:16]), AF.Copy, scale=P(11))
-    E("s", S.activation, ["it", "ps14"], ["wi"], T.wi[:], T.it[:], AF.Copy, scale=P(14))
-    if passes:
-        copy(["xb", "oxn"], ["xu"], T.xu[:], T.xb[:, 0:512].indirect(T.oxn[:, 0:32]))
-        copy(["xb", "oxg"], ["xg"], T.xg[:], T.xb[:, 0:512].indirect(T.oxg[:, 0:16]))
     copy(["spi"], ["spf"], T.spf[:], T.spi[:])
-    ts(["one", "spf"], ["spm"], T.spm[:], T.one[0:32, :], T.spf[:, 0:1], A.mult)
+    tp(["tkf"], ["blo"], T.blo[:], T.tkf[:])
+    ts(["tkf", "spf"], ["spm"], T.spm[:], T.tkf[0:32, :], 0.0, A.mult, T.spf[:, 0:1], A.add)
+    copy(["blo", "mo"], ["m0"], T.m0[:], T.blo[:, 0:32].indirect(T.mo[:, 0:32]))
     tp(["spm"], ["spb"], T.spb[:], T.spm[:])
+    tp(["m0"], ["xb"], T.xb[:], T.m0[:])
+    if passes:
+        act(["xb", "oxg"], ["xg"], T.xg[:], T.xb[:, 0:512].indirect(T.oxg[:, 0:16]))
+    act(["xb", "ovk", "ps11"], ["vk"], T.vk[:], T.xb[:, 0:512].indirect(T.ovk[:, 0:16]), scale=P(11))
+    act(["vc", "ps10", "ps16"], ["vd"], T.vd[:], T.vc[:], AF.Identity, scale=P(10), bias=P(16))
+    act(["it", "ps14"], ["wi"], T.wi[:], T.it[:], scale=P(14))
+    act(["it"], ["w2"], T.w2[:], T.it[:, 0:976], scale=0.0)
+    act(["it"], ["yfz"], T.yf[:, 0:16], T.it[:, 0:16], scale=0.0)
     for e in range(N - 1):
         ts(["blo", "spb"], ["d7"], T.d7[:, e:112:7], T.blo[0:32, 0:16], T.spb[:, e:e + 1], A.is_ge, 96.0, A.mult, add=True)
+    if passes:
+        copy(["xb", "oxn"], ["xu"], T.xu[:], T.xb[:, 0:512].indirect(T.oxn[:, 0:32]))
     scan(["d7", "rs7"], ["d7s"], T.d7s[:], T.rs7[:], T.d7[:], 0.0, A.mult, A.add)
+    tt(["vk", "vd"], ["val"], T.val[:], T.vk[:], T.vd[:], A.add)
     copy(["d7s"], ["d96"], T.d96[:, 0:16], T.d7s[:, 6:112:7])
-    ts(["itr", "ps"], ["tr"], T.tr[:], T.itr[:], T.ps[0:32, 0:1], A.add)
-    ts(["vc", "ps7", "ps10"], ["vc"], T.vc[:], T.vc[:], P(7), A.add, P(10), A.mult)
-    tt(["vk", "vc"], ["val"], T.val[:], T.vk[:], T.vc[:], A.add)
+    fill(["rs160"], T.rs160[:], 1.0)
+
+    later += [
+        lambda: ts(["ps", "ps3"], ["ps5"], P(5), P(2), 160.0, A.mult, P(3), A.add),
+        lambda: ts(["ps"], ["ps6"], P(6), P(1), 16.0, A.mult),
+        lambda: ts(["ps"], ["ps9"], P(9), P(2), 6.0, A.mult, P(0), A.add),
+        lambda: ts(["ps", "ps6"], ["ps15"], P(15), P(2), 160.0, A.mult, P(6), A.add),
+        lambda: ts(["ps"], ["ps8"], P(8), P(2), 2.0, A.mult),
+        lambda: ts(["ps"], ["ps13"], P(13), P(0), 2.0, A.is_equal),
+        lambda: ts(["ps"], ["ps12"], P(12), P(0), 1.0, A.is_equal),
+        lambda: ts(["ps15", "ps10"], ["ps17"], P(17), P(15), P(10), A.mult),
+        lambda: ts(["ps9"], ["ox6"], T.ox6[:, 0:1], P(9), 23.0, A.min),
+        lambda: ts(["ps8", "ps13", "ps12"], ["ps18"], P(18), P(8), P(13), A.mult, P(12), A.subtract),
+        lambda: ts(["ikg", "ps5"], ["okg"], T.okg[:], T.ik[:, 0:6], P(5), A.add),
+        lambda: fill(["rs160"], T.rs160[:, 0:640:160], 0.0)]
 
     if passes:
         tot["rk"] = 2 * (N - 1 - s)
@@ -185,47 +211,68 @@ def rank_program(g, core, T, topo):
         for h in H: ts(["cs" + h], ["of" + h], T["of" + h][:], T["cs" + h][:, 31:512:32], 1.0, A.subtract, 0.0, A.max)
         for i, h in enumerate(H):
             tt(["ta" + h, "of" + h, "xg"], ["eq"], T.eq[:, 256 * i:256 * i + 256], T["ta" + h][:, 0:32].indirect(T["of" + h][:, 0:16]), T.xg[:], A.is_equal, add=True)
+        gap()
         n = 256 * len(H)
         tp(["eq"], ["et"], T.et[:, 0:n], T.eq[:, 0:n])
+        gap()
         scan(["et", "rs16"], ["es"], T.es[:, 0:n], T.rs16[:, 0:n], T.et[:, 0:n], 0.0, A.mult, A.add)
+        gap()
         if len(H) == 2: tt(["es"], ["s0"], T.s0[:], T.es[:, 15:256:16], T.es[:, 271:512:16], A.add)
         else: copy(["es"], ["s0"], T.s0[:], T.es[:, 15:256:16])
+        gap()
         quads = list(range(min(first.values()), 4))
+        nq = len(quads)
+        C4 = lambda i: T.c4[:, 16 * i:16 * i + 16]
         for i, a in enumerate(quads):
-            copy(["s0"], ["c4"], T.c4[:, 16 * i:16 * i + 16], T.s0[32 * a:32 * a + 32, :], add=True)
-        if len(quads) == 4:
+            at = [0, 2, 1, 3][i] if nq == 4 else i
+            if i < (nq + 1) // 2: copy(["s0"], ["c4"], C4(at), T.s0[32 * a:32 * a + 32, :], add=True)
+            else: ts(["s0"], ["c4"], C4(at), T.s0[32 * a:32 * a + 32, :], -1.0, A.mult, add=True)
+        if nq == 4:
             tt(["c4"], ["a2"], T.a2[:], T.c4[:, 0:32], T.c4[:, 32:64], A.add)
-            tt(["a2"], ["fs"], T.fs[:], T.a2[:, 0:16], T.a2[:, 16:32], A.add)
-        elif len(quads) == 3:
-            tt(["c4"], ["a2"], T.a2[:, 0:16], T.c4[:, 0:16], T.c4[:, 16:32], A.add)
-            tt(["a2", "c4"], ["fs"], T.fs[:], T.a2[:, 0:16], T.c4[:, 32:48], A.add)
-        elif len(quads) == 2:
-            tt(["c4"], ["fs"], T.fs[:], T.c4[:, 0:16], T.c4[:, 16:32], A.add)
+            gap()
+            x, y, r = T.a2[:, 0:16], T.a2[:, 16:32], ["a2"]
+        elif nq == 3:
+            tt(["c4"], ["a2"], T.a2[:, 0:16], C4(0), C4(1), A.add)
+            gap()
+            x, y, r = T.a2[:, 0:16], C4(2), ["a2", "c4"]
         else:
-            copy(["c4"], ["fs"], T.fs[:], T.c4[:, 0:16])
-        ts(["fs"], ["kb"], T.kb[:, 1:17], T.fs[:], 0.0, A.is_equal)
-        ts(["fs"], ["f1"], T.f1[:], T.fs[:], 0.0, A.is_gt)
+            x, y, r = C4(0), C4(1), ["c4"]
+        if nq == 1:
+            ts(r, ["kb"], T.kb[:, 1:17], x, 0.0, A.is_equal)
+            ts(r, ["f1"], T.f1[:], x, 0.0, A.is_gt)
+        else:
+            tt(r, ["kb"], T.kb[:, 1:17], x, y, A.is_equal)
+            tt(r, ["f1"], T.f1[:], x, y, A.not_equal)
     scan(["kb", "zz"], ["pl"], T.pl[:, 0:17], T.kb[:, 0:17], T.zz[:, 0:17], 0.0, A.add, A.add)
     scan(["kb", "d96"], ["pl"], T.pl[:, 32:49], T.kb[:, 0:17], T.d96[:, 0:17], 0.0, A.add, A.max, add=True)
+    gap()
     tp(["pl"], ["pt"], T.pt[:], T.pl[:])
-    scan(["pt"], ["cc"], T.cc[:, 1:33], T.pt[:, 0:32], T.pt[:, 32:64], 0.0, A.add, A.max)
     if passes: tt(["f1", "tr"], ["nk"], T.nk[:], T.f1[:], T.tr[:], A.mult)
+    scan(["pt"], ["cc"], T.cc[:, 1:33], T.pt[:, 0:32], T.pt[:, 32:64], 0.0, A.add, A.max)
+    gap()
     tp(["cc"], ["cy"], T.cy[:], T.cc[:, 0:32])
+    gap()
     scan(["kb", "d96", "cy"], ["pq"], T.pq[:], T.kb[:, 0:16], T.d96[:, 0:16], T.cy[:, 16:17], A.add, A.max)
+    gap()
     src, tok = T.pq, "pq"
     if passes:
         tt(["pq", "nk"], ["pf"], T.pf[:], T.pq[:], T.nk[:], A.max)
+        gap()
         src, tok = T.pf, "pf"
     for a in range(4):
         copy([tok], ["pw"], T.pw[32 * a:32 * a + 32, :], src[:], add=True)
-    E("v", V.tensor_copy, ["pw", "val"], ["wi"], T.wi[:, 0:1024].indirect(T.pw[:, 0:16]), T.val[:])
+    E("v", V.tensor_copy, ["pw", "val"], ["wi"], T.wi[:, 0:1040].indirect(T.pw[:, 0:16]), T.val[:])
+    gap()
     tp(["wi"], ["wt"], T.wt[:], T.wi[:, 0:768])
+    gap()
     tt(["wt"], ["qk"], T.qk[:], T.wt[:, 1:768:32], T.wt[:, 17:768:32], A.max)
     tt(["wt"], ["qi"], T.qi[:, 0:24], T.wt[:, 0:768:32], T.wt[:, 16:768:32], A.max)
     peers = [(s + i) % N for i in range(1, N)]
     fused([(T.cores[d], T.kx[:, 3 * s:3 * s + 3], T.qk[:, 3 * d:3 * d + 3]) for d in peers], "rx", 2, ["qk"])
     D("y", "dkx", T.kx[:, 3 * s:3 * s + 3], T.qk[:, 3 * s:3 * s + 3], ["qk"], ["kx"], "par")
+    gap()
     tp(["qi"], ["xt"], T.xt[:], T.qi[:])
+    gap()
     for k in range(4):
         copy(["xt"], ["yy"], T.yy[:, 16 * k:16 * k + 16], T.xt[:, 16 * (k // 2):16 * (k // 2) + 16], add=True)
     tp(["yy"], ["ot"], T.ot[:], T.yy[:])
@@ -233,7 +280,7 @@ def rank_program(g, core, T, topo):
     copy(["ot"], ["off"], T.off[:, 1:48:2], T.ot[:, 32:56], add=True)
     def pick(d, cbuf, sbuf, c, tc, tz):
         E("v", V.tensor_copy, ["off", "kcs"], [tc], cbuf[:, c:c + 80].bitcast(dt.uint32), T.kcs[:, 0:512].bitcast(dt.uint32).indirect(T.off[:, 6 * d:6 * d + 5]))
-        E("s", S.activation, ["off", "kss"], [tz], sbuf[:, c:c + 80], T.kss[:, 0:512].indirect(T.off[:, 6 * d:6 * d + 5]), AF.Copy)
+        act(["off", "kss"], [tz], sbuf[:, c:c + 80], T.kss[:, 0:512].indirect(T.off[:, 6 * d:6 * d + 5]))
     for d in peers: pick(d, T.qc, T.qs, 80 * d, "qc%d" % d, "qs%d" % d)
     pick(s, T.lc, T.ls, 16 + 80 * s, "lco", "lso")
     me = 16 + 80 * s
@@ -244,63 +291,71 @@ def rank_program(g, core, T, topo):
         for r in part:
             tot["rc"] += e
             tot["rs"] += e
+    gap(len(later))
+    act(["ico", "ps17", "ps10"], ["ico2"], T.ico[:, 96:192], T.ico[:, 0:96], AF.Identity, scale=P(10), bias=P(17))
+    act(["irk", "ps18", "ps13"], ["irk2"], T.irk[:, 96:192], T.irk[:, 0:96], AF.Identity, scale=P(13), bias=P(18))
+    E("v", V.quantize_mx, ["wb"], ["wc", "wz"], T.wc[:], T.wz[:], T.wb[:])
+    tt(["ico2", "irk2"], ["cst"], T.cst[:], T.ico[:, 96:192], T.irk[:, 96:192], A.add)
     fill(["zb"], T.zb[:], 0.0)
-    fill(["sr"], T.sr[:], 0.0)
-    fill(["k2"], T.k2[:], 0.0)
     E("v", V.quantize_mx, ["zb"], ["zc", "zs"], T.zc[:], T.zs[:], T.zb[:])
     D("y", "dz", T.lc[:, 0:1].bitcast(dt.uint8), T.zc[:, 0:1].bitcast(dt.uint8), ["zc"], ["lcz"], "par")
     D("y", "dz", T.ls[:, 0:1], T.zs[:, 0:1], ["zs"], ["lsz"], "par")
-    fill(["w2"], T.w2[:], 0.0)
-    fill(["yfz"], T.yf[:, 0:16], 0.0)
-    ts(["ps", "ps3"], ["ps5"], P(5), P(2), 160.0, A.mult, P(3), A.add)
-    ts(["ps"], ["ps6"], P(6), P(1), 16.0, A.mult)
-    ts(["ps"], ["ps8"], P(8), P(2), 2.0, A.mult)
-    ts(["ps"], ["ps9"], P(9), P(2), 6.0, A.mult, P(0), A.add)
-    ts(["ps"], ["ps12"], P(12), P(0), 1.0, A.is_equal)
-    ts(["ps"], ["ps13"], P(13), P(0), 2.0, A.is_equal)
-    ts(["ps", "ps6"], ["ps15"], P(15), P(2), 160.0, A.mult, P(6), A.add)
-    ts(["ps9"], ["ox6"], T.ox6[:, 0:1], P(9), 23.0, A.min)
-    ts(["ikg", "ps5"], ["okg"], T.okg[:], T.ik[:, 0:6], P(5), A.add)
-    ts(["ico", "ps15", "ps10"], ["ico"], T.ico[:], T.ico[:], P(15), A.add, P(10), A.mult)
-    ts(["irk", "ps8", "ps13"], ["irk"], T.irk[:], T.irk[:], P(8), A.add, P(13), A.mult)
-    tt(["ico", "irk"], ["cst"], T.cst[:], T.ico[:], T.irk[:], A.add)
-    ts(["cst", "ps12"], ["cst"], T.cst[:], T.cst[:], P(12), A.subtract)
-    ts(["ijt", "ps"], ["jf"], T.jf[:], T.ik[:, 6:12], P(0), A.add)
-    E("v", V.quantize_mx, ["wb"], ["wc", "wz"], T.wc[:], T.wz[:], T.wb[:])
     tot["rx"] = 2 * (N - 1)
     wr["rx"] = [("rx", None)]
-    E("s", S.activation, ["rx", "kx", "mo"], ["mmS"], T.mm[:, 384:768], T.kx[:, 0:24].indirect(T.mo[:, 24:48]), AF.Copy)
-    copy(["rx", "kx", "mo"], ["mmV"], T.mm[:, 0:384], T.kx[:, 0:24].indirect(T.mo[:, 0:24]))
+    act(["rx", "kx", "mo"], ["mmS"], T.mm[:, 384:768], T.kx[:, 0:24].indirect(T.mo[:, 24:48]))
     copy(["rx", "kx", "ox6"], ["x6"], T.x6[:], T.kx[:, 0:24].indirect(T.ox6[:, 0:1]))
+    copy(["rx", "kx", "mo"], ["mmV"], T.mm[:, 0:384], T.kx[:, 0:24].indirect(T.mo[:, 0:24]))
     ts(["x6"], ["nx6"], T.nx6[:], T.x6[:], -1.0, A.mult)
     for r in range(N):
         tp(["mmV" if r < 4 else "mmS"], ["xf3"], T.xf[:, 80 * r + 64:80 * r + 96], T.mm[:, 96 * r + 64:96 * r + 96], add=True)
+    ts(["x6"], ["pd"], T.pd[:], T.x6[:, 0:6], -65536.0, A.is_lt)
     for r in range(N):
         tp(["mmV" if r < 4 else "mmS", "xf3"], ["xf"], T.xf[:, 80 * r:80 * r + 64], T.mm[:, 96 * r:96 * r + 64], add=True)
     for e in range(4):
-        E("s", S.activation, ["xf", "xf3", "nx6"], ["jk%d" % e, "sm%d" % e], T.jk[:, 640 * e:640 * e + 640], T.xf[:, 0:640], AF.Sign, bias=T.nx6[:, e:e + 1], accum_out=T.sm[:, e:e + 1])
-    ts(["xf", "xf3", "okg", "ps12"], ["kg"], T.kg[:], T.xf[:, 0:656].indirect(T.okg[:, 0:6]), P(12), A.mult)
-    ts(["xf", "x6"], ["cb0"], T.cb0[:], T.xf[:, 0:640], T.x6[:, 4:5], A.is_gt)
-    ts(["xf", "x6"], ["cb1"], T.cb1[:], T.xf[:, 0:640], T.x6[:, 5:6], A.is_gt)
-    tt(["kg", "cst"], ["va2"], T.va2[:], T.kg[:], T.cst[:], A.add)
-    ts(["x6"], ["pd"], T.pd[:], T.x6[:, 0:6], -65536.0, A.is_lt)
+        act(["xf", "xf3", "nx6"], ["jk%d" % e, "sm%d" % e], T.jk[:, 640 * e:640 * e + 640], T.xf[:, 0:640], AF.Sign, bias=T.nx6[:, e:e + 1], accum_out=T.sm[:, e:e + 1])
+    tt(["pd", "jf", "jf2"], ["jt0"], T.jt[:, 6:12], T.pd[:], T.jf[:], A.mult)
     for k in (0, 1):
-        E("v", V.tensor_reduce, ["cb%d" % k], ["p6%d" % k], T.p6[:, 4 + k:5 + k], T["cb%d" % k][:], AxisListType.X, A.add)
-    tt(["pd", "jf"], ["jt"], T.jt[:], T.pd[:], T.jf[:], A.mult)
-    ts(["sm%d" % e for e in range(4)], ["p6"], T.p6[:, 0:4], T.sm[:], 639.0, A.add, 0.5, A.mult)
-    tt(["p6", "p60", "p61", "jt"], ["p6b"], T.p6b[:], T.p6[:, 0:6], T.jt[:], A.max)
-    copy(["p6b"], ["pu"], T.pu[:], T.p6b[:])
-    E("v", V.tensor_copy, ["pu", "va2"], ["w2"], T.w2[:, 0:896].indirect(T.pu[:, 0:6]), T.va2[:], add=True)
+        ts(["xf", "xf3", "x6"], ["cb%d" % k], T.cb[:, 640 * k:640 * k + 640], T.xf[:, 0:640], T.x6[:, 4 + k:5 + k], A.is_gt)
+    ts(["xf", "xf3", "okg", "ps12"], ["kg"], T.kg[:], T.xf[:, 0:656].indirect(T.okg[:, 0:6]), P(12), A.mult)
+    for k in (0, 1):
+        scan(["cb%d" % k, "rs160"], ["cbs%d" % k], T.cbs[:, 640 * k:640 * k + 640], T.rs160[:], T.cb[:, 640 * k:640 * k + 640], 0.0, A.mult, A.add)
+    tt(["kg", "cst"], ["va2"], T.va2[:], T.kg[:], T.cst[:], A.add)
+    ts(["jt0"], ["jt"], T.jt[:, 0:6], T.jt[:, 6:12], 10000.0, A.subtract)
+    for k in (0, 1):
+        E("v", V.tensor_reduce, ["cbs%d" % k], ["sm%d" % (4 + k)], T.sm[:, 4 + k:5 + k], T.cbs[:, 640 * k + 159:640 * k + 640:160], AxisListType.X, A.add)
+    tt(["sm%d" % e for e in range(6)] + ["jt"], ["pm"], T.pm[:], T.sm[:], T.jt[:, 0:6], A.max)
+    ts(["pm"], ["pu"], T.pu[:, 0:4], T.pm[:, 0:4], 639.0, A.add, 0.5, A.mult)
+    copy(["pm"], ["pu"], T.pu[:, 4:6], T.pm[:, 4:6], add=True)
+    E("v", V.tensor_copy, ["pu", "va2"], ["w2"], T.w2[:, 0:976].indirect(T.pu[:, 0:6]), T.va2[:])
     tp(["w2"], ["w2t"], T.w2t[:], T.w2[:, 0:512])
+    def ok_rows():
+        tp(["k2"], ["ro"], T.ro[:], T.k2[:])
+        D("y", "dok", T.ok[0:1, :], T.ro[0:16, 0:32], ["ro"], ["ok"], "par")
+        D("y", "dok", T.ok[1:2, :], T.ro[0:16, 32:64], ["ro"], ["ok"], "par")
+    later += [lambda k=k: tt(["w2t"], ["t3k"], T.t3[:, 16 * k:16 * k + 16], T.w2t[:, k:512:32], T.w2t[:, 16 + k:512:32], A.add, add=True) for k in (1, 2)]
+    later += [lambda a=a: copy(["t3k"], ["c6"], T.c6[:, 32 * a:32 * a + 32], T.t3[32 * a:32 * a + 32, 16:48], add=True) for a in range(4)]
+    later += [
+        lambda: tt(["c6"], ["a6"], T.a6[:], T.c6[:, 0:64], T.c6[:, 64:128], A.add),
+        lambda: tt(["a6"], ["c6b"], T.c6[:, 0:32], T.a6[:, 0:32], T.a6[:, 32:64], A.add),
+        lambda: ts(["c6b"], ["k2"], T.k2[:, 0:16], T.c6[:, 0:16], -1.0, A.mult, 1.0, A.subtract),
+        lambda: ts(["c6b"], ["k2"], T.k2[:, 32:48], T.c6[:, 16:32], 1.0, A.subtract, add=True),
+        ok_rows]
     tt(["w2t"], ["t3"], T.t3[:, 0:16], T.w2t[:, 0:512:32], T.w2t[:, 16:512:32], A.add)
+    gap()
     for a in range(4):
         copy(["t3"], ["c5"], T.c5[:, 16 * a:16 * a + 16], T.t3[32 * a:32 * a + 32, 0:16], add=True)
+    gap()
     tt(["c5"], ["a5"], T.a5[:], T.c5[:, 0:32], T.c5[:, 32:64], A.add)
+    gap()
     tt(["a5"], ["sr"], T.sr[:, 0:16], T.a5[:, 0:16], T.a5[:, 16:32], A.add)
+    gap()
     tp(["sr"], ["sx"], T.sx[:], T.sr[:])
+    gap()
     for k in range(4):
         copy(["sx"], ["sy"], T.sy[:, 16 * k:16 * k + 16], T.sx[:, 16 * (k // 2):16 * (k // 2) + 16], add=True)
+    gap()
     tp(["sy"], ["so"], T.so[:], T.sy[:])
+    gap()
     for a in range(4):
         copy(["so"], ["of2"], T.of2[32 * a:32 * a + 32, 0:32:2], T.so[:, 0:16], add=True)
         copy(["so"], ["of2"], T.of2[32 * a:32 * a + 32, 1:32:2], T.so[:, 32:48], add=True)
@@ -310,31 +365,21 @@ def rank_program(g, core, T, topo):
         c = 16 + 320 * k
         E("t", g.tensor.matmul_mx, land + lands + ["wc", "wz"], ["acc%d" % k], T.acc[:, 512 * k:512 * k + 320], T.wc[:], T.wz[:], T.lc[:, c:c + 320], T.ls[:, c:c + 320], True, True)
     for k in (0, 1):
-        E("s", S.activation, ["acc%d" % k], ["yf%d" % k], T.yf[:, 16 + 320 * k:336 + 320 * k], T.acc[:, 512 * k:512 * k + 320], AF.Copy)
+        act(["acc%d" % k], ["yf%d" % k], T.yf[:, 16 + 320 * k:336 + 320 * k], T.acc[:, 512 * k:512 * k + 320])
     ys = ["yfz", "yf0", "yf1", "of2"]
     def codes(k):
         E("v", V.tensor_copy, land + ["of2"], ["fc%d" % k], T.fc[:, 256 * k:256 * k + 256].bitcast(dt.uint32), T.lc[:, 0:656].bitcast(dt.uint32).indirect(T.of2[:, 16 * k:16 * k + 16]))
         D("y", ["doc", "doc2"][k], T.oc[:, 1024 * k:1024 * k + 1024], T.fc[:, 256 * k:256 * k + 256].bitcast(dt.uint8), ["fc%d" % k], ["oc"], "par")
     codes(0)
-    E("s", S.activation, ys, ["yo0"], T.yo[:, 0:256], T.yf[:, 0:656].indirect(T.of2[:, 0:16]), AF.Copy)
+    act(ys, ["yo0"], T.yo[:, 0:256], T.yf[:, 0:656].indirect(T.of2[:, 0:16]))
     D("y", "dy", T.y[:, 0:256], T.yo[:, 0:256], ["yo0"], ["y"], "par")
     codes(1)
-    E("s", S.activation, lands + ["of2"], ["fz"], T.fz[:], T.ls[:, 0:656].indirect(T.of2[:, 0:32]), AF.Copy)
+    act(lands + ["of2"], ["fz"], T.fz[:], T.ls[:, 0:656].indirect(T.of2[:, 0:32]))
     for k in range(4):
         D("s", "dos", T.osc[4 * k:4 * k + 4, :], T.fz[32 * k:32 * k + 4, :], ["fz"], ["osc"], "par")
     copy(ys, ["yo1"], T.yo[:, 256:512], T.yf[:, 0:656].indirect(T.of2[:, 16:32]))
     D("y", "dy2", T.y[:, 256:512], T.yo[:, 256:512], ["yo1"], ["y"], "par")
-    tt(["w2t"], ["t3k"], T.t3[:, 16:32], T.w2t[:, 1:512:32], T.w2t[:, 17:512:32], A.add)
-    tt(["w2t"], ["t3k"], T.t3[:, 32:48], T.w2t[:, 2:512:32], T.w2t[:, 18:512:32], A.add, add=True)
-    for a in range(4):
-        copy(["t3k"], ["c6"], T.c6[:, 32 * a:32 * a + 32], T.t3[32 * a:32 * a + 32, 16:48], add=True)
-    tt(["c6"], ["a6"], T.a6[:], T.c6[:, 0:64], T.c6[:, 64:128], A.add)
-    tt(["a6"], ["c6b"], T.c6[:, 0:32], T.a6[:, 0:32], T.a6[:, 32:64], A.add)
-    ts(["c6b"], ["k2"], T.k2[:, 0:16], T.c6[:, 0:16], -1.0, A.mult, 1.0, A.subtract, add=True)
-    ts(["c6b"], ["k2"], T.k2[:, 32:48], T.c6[:, 16:32], 1.0, A.subtract, add=True)
-    tp(["k2"], ["ro"], T.ro[:], T.k2[:])
-    D("y", "dok", T.ok[0:1, :], T.ro[0:16, 0:32], ["ro"], ["ok"], "par")
-    D("y", "dok", T.ok[1:2, :], T.ro[0:16, 32:64], ["ro"], ["ok"], "par")
+    gap(len(later))
     for n in SEMAPHORES:
         if tot[n]:
             g.wait_ge(T.sem[n], tot[n])

@@ -4,20 +4,20 @@ from concourse.mybir import dt, AluOpType, AxisListType, ActivationFunctionType
 SCRATCH = {"mykd": ("dram", [128, 8], "int32"), "kd0": ("dram", [4, 128, 8], "int32"), "kd1": ("dram", [4, 128, 8], "int32"),
            "acc": ("psum", [128, 1024], "float32")}
 SIZES = {
-    (128, "float32"): "tkf:32 blo:32 m0:512 xb:512 xg:256 val:256 vk:256 vc:256 vd:256 ta0:32 ta1:32 bl0:32 bl1:32 ps:32 it:1040 ix:112 ik:6 ico:192 irk:192 "
-                      "cst:96 jf:6 pd:6 jt:12 s0:16 wi:1040 wt:768 qk:24 qi:32 xt:32 yy:64 ot:64 kx:24 mm:768 xf:672 x6:16 nx6:16 sm:6 "
-                      "pm:6 kg:96 va2:96 w2:976 w2t:512 t3:48 yf:656 yo:512",
+    (128, "float32"): "tkf:32 blo:32 m0:512 xb:512 xg:256 val:256 vk:256 vc:256 vd:256 ta0:32 ta1:32 bl0:32 bl1:32 ps:32 it:1040 ix:112 im:80 mh:40 ico:160 irk:240 "
+                      "cst:80 jf:5 pd:5 jt:10 s0:16 wi:1040 wt:768 qk:24 qi:32 xt:32 yy:64 ot:64 kx:24 mm:640 xf:640 x6:16 nx6:16 sm:5 "
+                      "pm:5 kg:80 va2:80 w2:960 w2t:512 t3:48 sr:32 sx:32 sy:64 so:64 yf:656 yo:512",
     (32, "float32"): "tr:16 spf:1 spm:32 spb:32 d7:112 d7s:112 rs7:112 d96:20 c4:64 a2:32 kb:20 f1:16 nk:16 zz:20 pl:64 pt:64 cc:64 cy:32 "
-                     "pq:16 pf:16 c5:64 a5:32 sr:32 sx:32 sy:64 so:64 c6:128 a6:64 k2:64 ro:64",
-    (128, "bfloat16"): "cm0:512 cm1:512 ct0:512 ct1:512 cs0:512 cs1:512 eq:512 et:512 es:512 rs32:512 rs16:512 rs160:640 zb:512 wb:512 jk:2560 cb:1280 cbs:1280",
+                     "pq:16 pf:16 c5:64 a5:32 c6:128 a6:64 k2:32 ro:32",
+    (128, "bfloat16"): "cm0:512 cm1:512 ct0:512 ct1:512 cs0:512 cs1:512 eq:512 et:512 es:512 rs32:512 rs16:512 rs160:640 zb:512 wb:512 jk:1920 cb:1280 cbs:1280",
     (128, "int32"): "tk:32 ti0:32 ti1:32 pi:8", (32, "int32"): "spi:1",
-    (128, "uint16"): "xu:512 of0:16 of1:16 mo:48 oxn:32 oxg:16 ovk:16 okg:6 ox6:2 pw:16 off:48 pu:6 of2:32",
+    (128, "uint16"): "xu:512 of0:16 of1:16 mb:32 mo:40 oxn:32 oxg:16 ovk:16 okg:6 ox6:2 pw:16 off:48 pu:6 of2:32",
     (128, "float8_e4m3fn_x4"): "zc:128 kcs:512 qc:640 lc:656 fc:512 wc:128",
     (128, "uint8"): "zs:128 kss:512 qs:640 ls:672 fz:512 wz:128"}
 for (_p, _d), _l in SIZES.items():
     for _x in _l.split():
         SCRATCH[_x.split(":")[0]] = ("sbuf", [_p, int(_x.split(":")[1])], _d)
-SEMAPHORES = ["vs", "ss", "ts", "gs", "dk", "dt", "dsp", "dw", "dkc", "dz", "dta", "dtb", "dkx", "doc", "doc2", "dos", "dy", "dy2", "dok",
+SEMAPHORES = ["vs", "ss", "ts", "gs", "dk", "dt", "dsp", "dw", "dkc", "dz", "dta", "dtb", "dkx", "doc", "doc2", "dos", "dy", "dy2", "dy3", "dok",
               "rk", "rx", "rc", "rs", "loc"]
 
 
@@ -98,6 +98,7 @@ def rank_program(g, core, T, topo):
 
     passes = [h for h in (0, 1) if any(2 * a + h > s for a in range(4))]
     first = {h: min(a for a in range(4) if 2 * a + h > s) for h in passes}
+    odd = s % 2
 
     if s > 0:
         for k in (0, 1):
@@ -111,27 +112,29 @@ def rank_program(g, core, T, topo):
     D("y", "dw", T.wb[:], T.w[:], [], ["wb"], "par")
 
     iota(["pi"], T.pi[:, 0:1], [[0, 1]], 0, 1)
-    iota(["imo"], T.ix[:, 0:48], [[1, 24], [0, 2]], 0)
+    iota(["imb"], T.ix[:, 0:32], [[1, 16], [0, 2]], 0)
     iota(["ixn"], T.ix[:, 48:80], [[64, 8], [16, 2], [32, 2]], 0)
     iota(["ixg"], T.ix[:, 80:96], [[64, 8], [16, 2]], 0)
     iota(["ivk"], T.ix[:, 96:112], [[32, 16]], 0)
     if s > 0:
-        fused([(T.cores[r], T["kd%d" % (s % 2)][s // 2], T.mykd[:]) for r in range(s)], "rk", 2, ["mykd"])
+        fused([(T.cores[r], T["kd%d" % odd][s // 2], T.mykd[:]) for r in range(s)], "rk", 1, ["mykd"])
     iota(["vc"], T.vc[:], [[1, 16], [16, 16]], 0)
-    iota(["it"], T.it[:], [[-1, 1040]], -(66000 + 768 * s))
     iota(["d96"], T.d96[:], [[0, 20]], 0)
-    iota(["tr"], T.tr[:], [[16, 16]], 768, 1)
     if not passes:
         iota(["kb"], T.kb[:], [[0, 20]], 1)
     iota(["kb"], T.kb[:, 0:1], [[0, 1]], 0)
+    iota(["im2"], T.im[:, 40:80], [[0, 4], [1, 5], [0, 2]], 0)
+    iota(["im"], T.im[:, 0:40], [[6, 4], [1, 5], [0, 2]], 0)
+    iota(["tr"], T.tr[:], [[16, 16]], 768, 1)
     for n, c in (("zz", 20), ("pl", 64), ("cc", 64), ("qi", 32)):
         iota([n], T[n][:], [[0, c]], 0)
-    iota(["ikg"], T.ik[:, 0:6], [[80, 2], [32, 3]], 0)
-    iota(["ico"], T.ico[:, 0:96], [[80, 2], [32, 3], [1, 16]], 16)
-    iota(["irk"], T.irk[:, 0:96], [[1, 2], [0, 48]], 1)
-    iota(["jf"], T.jf[:, 0:4], [[32, 4]], 10897, 2)
-    iota(["jf2"], T.jf[:, 4:6], [[16, 2]], 10832, 1)
-    for n, c in (("sr", 32), ("k2", 64)):
+    iota(["ikg"], T.ix[:, 32:37], [[32, 5]], 0)
+    iota(["irk"], T.irk[:, 0:80], [[1, 5], [0, 16]], 0)
+    iota(["it"], T.it[:], [[-1, 1040]], -(66000 + 768 * s))
+    iota(["ico"], T.ico[:, 0:80], [[32, 5], [1, 16]], 16)
+    iota(["jf"], T.jf[:, 0:3], [[32, 3]], 10897, 2)
+    iota(["jf2"], T.jf[:, 3:5], [[16, 2]], 10816, 1)
+    for n, c in (("sr", 32), ("k2", 32)):
         iota([n], T[n][:], [[0, c]], 0)
 
     for h in passes:
@@ -144,7 +147,7 @@ def rank_program(g, core, T, topo):
     fill(["rs7"], T.rs7[:], 1.0)
     copy(["pi1", "pi2", "pi3"], ["ps"], T.ps[:, 0:3], T.pi[:, 1:4])
     P = lambda k: T.ps[:, k:k + 1]
-    copy(["imo"], ["mo"], T.mo[:], T.ix[:, 0:48])
+    copy(["imb"], ["mb"], T.mb[:], T.ix[:, 0:32])
     fill(["rs16"], T.rs16[:], 1.0)
     ts(["ps"], ["ps3"], P(3), P(1), 16.0, A.mult, P(0), A.add)
     ts(["ps"], ["ps4"], P(4), P(1), 32.0, A.mult, P(0), A.add)
@@ -163,7 +166,7 @@ def rank_program(g, core, T, topo):
     copy(["spi"], ["spf"], T.spf[:], T.spi[:])
     tp(["tkf"], ["blo"], T.blo[:], T.tkf[:])
     ts(["tkf", "spf"], ["spm"], T.spm[:], T.tkf[0:32, :], 0.0, A.mult, T.spf[:, 0:1], A.add)
-    copy(["blo", "mo"], ["m0"], T.m0[:], T.blo[:, 0:32].indirect(T.mo[:, 0:32]))
+    copy(["blo", "mb"], ["m0"], T.m0[:], T.blo[:, 0:32].indirect(T.mb[:, 0:32]))
     tp(["spm"], ["spb"], T.spb[:], T.spm[:])
     tp(["m0"], ["xb"], T.xb[:], T.m0[:])
     if passes:
@@ -171,7 +174,7 @@ def rank_program(g, core, T, topo):
     act(["xb", "ovk", "ps11"], ["vk"], T.vk[:], T.xb[:, 0:512].indirect(T.ovk[:, 0:16]), scale=P(11))
     act(["vc", "ps10", "ps16"], ["vd"], T.vd[:], T.vc[:], AF.Identity, scale=P(10), bias=P(16))
     act(["it", "ps14"], ["wi"], T.wi[:], T.it[:], scale=P(14))
-    act(["it"], ["w2"], T.w2[:], T.it[:, 0:976], scale=0.0)
+    act(["it"], ["w2"], T.w2[:], T.it[:, 0:960], scale=0.0)
     act(["it"], ["yfz"], T.yf[:, 0:16], T.it[:, 0:16], scale=0.0)
     for e in range(N - 1):
         ts(["blo", "spb"], ["d7"], T.d7[:, e:112:7], T.blo[0:32, 0:16], T.spb[:, e:e + 1], A.is_ge, 96.0, A.mult, add=True)
@@ -179,25 +182,30 @@ def rank_program(g, core, T, topo):
         copy(["xb", "oxn"], ["xu"], T.xu[:], T.xb[:, 0:512].indirect(T.oxn[:, 0:32]))
     scan(["d7", "rs7"], ["d7s"], T.d7s[:], T.rs7[:], T.d7[:], 0.0, A.mult, A.add)
     tt(["vk", "vd"], ["val"], T.val[:], T.vk[:], T.vd[:], A.add)
-    copy(["d7s"], ["d96"], T.d96[:, 0:16], T.d7s[:, 6:112:7])
+    ts(["d7s"], ["d96"], T.d96[:, 0:16], T.d7s[:, 6:112:7], 16.0 * odd, A.add)
     fill(["rs160"], T.rs160[:], 1.0)
 
     later += [
-        lambda: ts(["ps", "ps3"], ["ps5"], P(5), P(2), 160.0, A.mult, P(3), A.add),
-        lambda: ts(["ps"], ["ps6"], P(6), P(1), 16.0, A.mult),
+        lambda: ts(["im2", "ps"], ["mh"], T.mh[:], T.im[:, 40:80], P(1), A.add, 3.0, A.is_ge),
+        lambda: ts(["ps"], ["ps18"], P(18), P(0), P(1), A.add, 3.0, A.is_ge),
         lambda: ts(["ps"], ["ps9"], P(9), P(2), 6.0, A.mult, P(0), A.add),
+        lambda: ts(["ps"], ["ps6"], P(6), P(1), 16.0, A.mult),
+        lambda: tt(["im", "mh"], ["mo"], T.mo[:], T.im[:, 0:40], T.mh[:], A.add),
+        lambda: ts(["ps", "ps3"], ["ps5"], P(5), P(2), 160.0, A.mult, P(3), A.add),
+        lambda: ts(["ps9", "ps18"], ["ps19"], P(19), P(9), P(18), A.add),
         lambda: ts(["ps", "ps6"], ["ps15"], P(15), P(2), 160.0, A.mult, P(6), A.add),
-        lambda: ts(["ps"], ["ps8"], P(8), P(2), 2.0, A.mult),
+        lambda: ts(["ps"], ["ps8"], P(8), P(2), 2.0, A.mult, 1.0, A.add),
+        lambda: ts(["ps19"], ["ox6"], T.ox6[:, 0:1], P(19), 23.0, A.min),
         lambda: ts(["ps"], ["ps13"], P(13), P(0), 2.0, A.is_equal),
-        lambda: ts(["ps"], ["ps12"], P(12), P(0), 1.0, A.is_equal),
+        lambda: ts(["ps"], ["ps12"], P(12), P(0), 1.0, A.is_equal, -1.0, A.mult),
         lambda: ts(["ps15", "ps10"], ["ps17"], P(17), P(15), P(10), A.mult),
-        lambda: ts(["ps9"], ["ox6"], T.ox6[:, 0:1], P(9), 23.0, A.min),
-        lambda: ts(["ps8", "ps13", "ps12"], ["ps18"], P(18), P(8), P(13), A.mult, P(12), A.subtract),
-        lambda: ts(["ikg", "ps5"], ["okg"], T.okg[:], T.ik[:, 0:6], P(5), A.add),
+        lambda: ts(["ikg", "ps5"], ["okg"], T.okg[:, 0:5], T.ix[:, 32:37], P(5), A.add),
+        lambda: ts(["irk", "ps"], ["irk1"], T.irk[:, 80:160], T.irk[:, 0:80], P(1), A.add, 3.0, A.is_ge),
+        lambda: ts(["ps8", "ps13", "ps12"], ["ps20"], P(20), P(8), P(13), A.mult, P(12), A.subtract),
         lambda: fill(["rs160"], T.rs160[:, 0:640:160], 0.0)]
 
     if passes:
-        tot["rk"] = 2 * (N - 1 - s)
+        tot["rk"] = N - 1 - s
         wr["rk"] = [("rk", None)]
         for h in passes:
             a = first[h]
@@ -211,7 +219,6 @@ def rank_program(g, core, T, topo):
         for h in H: ts(["cs" + h], ["of" + h], T["of" + h][:], T["cs" + h][:, 31:512:32], 1.0, A.subtract, 0.0, A.max)
         for i, h in enumerate(H):
             tt(["ta" + h, "of" + h, "xg"], ["eq"], T.eq[:, 256 * i:256 * i + 256], T["ta" + h][:, 0:32].indirect(T["of" + h][:, 0:16]), T.xg[:], A.is_equal, add=True)
-        gap()
         n = 256 * len(H)
         tp(["eq"], ["et"], T.et[:, 0:n], T.eq[:, 0:n])
         gap()
@@ -227,6 +234,7 @@ def rank_program(g, core, T, topo):
             at = [0, 2, 1, 3][i] if nq == 4 else i
             if i < (nq + 1) // 2: copy(["s0"], ["c4"], C4(at), T.s0[32 * a:32 * a + 32, :], add=True)
             else: ts(["s0"], ["c4"], C4(at), T.s0[32 * a:32 * a + 32, :], -1.0, A.mult, add=True)
+        gap()
         if nq == 4:
             tt(["c4"], ["a2"], T.a2[:], T.c4[:, 0:32], T.c4[:, 32:64], A.add)
             gap()
@@ -253,14 +261,15 @@ def rank_program(g, core, T, topo):
     tp(["cc"], ["cy"], T.cy[:], T.cc[:, 0:32])
     gap()
     scan(["kb", "d96", "cy"], ["pq"], T.pq[:], T.kb[:, 0:16], T.d96[:, 0:16], T.cy[:, 16:17], A.add, A.max)
-    gap()
     src, tok = T.pq, "pq"
+    gap()
     if passes:
         tt(["pq", "nk"], ["pf"], T.pf[:], T.pq[:], T.nk[:], A.max)
-        gap()
         src, tok = T.pf, "pf"
+        gap()
     for a in range(4):
         copy([tok], ["pw"], T.pw[32 * a:32 * a + 32, :], src[:], add=True)
+    gap()
     E("v", V.tensor_copy, ["pw", "val"], ["wi"], T.wi[:, 0:1040].indirect(T.pw[:, 0:16]), T.val[:])
     gap()
     tp(["wi"], ["wt"], T.wt[:], T.wi[:, 0:768])
@@ -275,9 +284,15 @@ def rank_program(g, core, T, topo):
     gap()
     for k in range(4):
         copy(["xt"], ["yy"], T.yy[:, 16 * k:16 * k + 16], T.xt[:, 16 * (k // 2):16 * (k // 2) + 16], add=True)
+    gap()
     tp(["yy"], ["ot"], T.ot[:], T.yy[:])
-    copy(["ot"], ["off"], T.off[:, 0:48:2], T.ot[:, 0:24])
-    copy(["ot"], ["off"], T.off[:, 1:48:2], T.ot[:, 32:56], add=True)
+    gap()
+    if odd:
+        copy(["ot"], ["off"], T.off[:, 0:48:2], T.ot[:, 32:56])
+        copy(["ot"], ["off"], T.off[:, 1:47:2], T.ot[:, 1:24], add=True)
+    else:
+        copy(["ot"], ["off"], T.off[:, 0:48:2], T.ot[:, 0:24])
+        copy(["ot"], ["off"], T.off[:, 1:48:2], T.ot[:, 32:56], add=True)
     def pick(d, cbuf, sbuf, c, tc, tz):
         E("v", V.tensor_copy, ["off", "kcs"], [tc], cbuf[:, c:c + 80].bitcast(dt.uint32), T.kcs[:, 0:512].bitcast(dt.uint32).indirect(T.off[:, 6 * d:6 * d + 5]))
         act(["off", "kss"], [tz], sbuf[:, c:c + 80], T.kss[:, 0:512].indirect(T.off[:, 6 * d:6 * d + 5]))
@@ -292,62 +307,62 @@ def rank_program(g, core, T, topo):
             tot["rc"] += e
             tot["rs"] += e
     gap(len(later))
-    act(["ico", "ps17", "ps10"], ["ico2"], T.ico[:, 96:192], T.ico[:, 0:96], AF.Identity, scale=P(10), bias=P(17))
-    act(["irk", "ps18", "ps13"], ["irk2"], T.irk[:, 96:192], T.irk[:, 0:96], AF.Identity, scale=P(13), bias=P(18))
+    act(["ico", "ps17", "ps10"], ["ico2"], T.ico[:, 80:160], T.ico[:, 0:80], AF.Identity, scale=P(10), bias=P(17))
+    act(["irk1", "ps20", "ps13"], ["irk2"], T.irk[:, 160:240], T.irk[:, 80:160], AF.Identity, scale=P(13), bias=P(20))
     E("v", V.quantize_mx, ["wb"], ["wc", "wz"], T.wc[:], T.wz[:], T.wb[:])
-    tt(["ico2", "irk2"], ["cst"], T.cst[:], T.ico[:, 96:192], T.irk[:, 96:192], A.add)
     fill(["zb"], T.zb[:], 0.0)
+    tt(["ico2", "irk2"], ["cst"], T.cst[:], T.ico[:, 80:160], T.irk[:, 160:240], A.add)
     E("v", V.quantize_mx, ["zb"], ["zc", "zs"], T.zc[:], T.zs[:], T.zb[:])
     D("y", "dz", T.lc[:, 0:1].bitcast(dt.uint8), T.zc[:, 0:1].bitcast(dt.uint8), ["zc"], ["lcz"], "par")
     D("y", "dz", T.ls[:, 0:1], T.zs[:, 0:1], ["zs"], ["lsz"], "par")
     tot["rx"] = 2 * (N - 1)
     wr["rx"] = [("rx", None)]
-    act(["rx", "kx", "mo"], ["mmS"], T.mm[:, 384:768], T.kx[:, 0:24].indirect(T.mo[:, 24:48]))
+    act(["rx", "kx", "mo"], ["mmS"], T.mm[:, 256:640], T.kx[:, 0:24].indirect(T.mo[:, 16:40]))
     copy(["rx", "kx", "ox6"], ["x6"], T.x6[:], T.kx[:, 0:24].indirect(T.ox6[:, 0:1]))
-    copy(["rx", "kx", "mo"], ["mmV"], T.mm[:, 0:384], T.kx[:, 0:24].indirect(T.mo[:, 0:24]))
+    copy(["rx", "kx", "mo"], ["mmV"], T.mm[:, 0:256], T.kx[:, 0:24].indirect(T.mo[:, 0:16]))
     ts(["x6"], ["nx6"], T.nx6[:], T.x6[:], -1.0, A.mult)
-    for r in range(N):
-        tp(["mmV" if r < 4 else "mmS"], ["xf3"], T.xf[:, 80 * r + 64:80 * r + 96], T.mm[:, 96 * r + 64:96 * r + 96], add=True)
-    ts(["x6"], ["pd"], T.pd[:], T.x6[:, 0:6], -65536.0, A.is_lt)
-    for r in range(N):
-        tp(["mmV" if r < 4 else "mmS", "xf3"], ["xf"], T.xf[:, 80 * r:80 * r + 64], T.mm[:, 96 * r:96 * r + 64], add=True)
-    for e in range(4):
-        act(["xf", "xf3", "nx6"], ["jk%d" % e, "sm%d" % e], T.jk[:, 640 * e:640 * e + 640], T.xf[:, 0:640], AF.Sign, bias=T.nx6[:, e:e + 1], accum_out=T.sm[:, e:e + 1])
-    tt(["pd", "jf", "jf2"], ["jt0"], T.jt[:, 6:12], T.pd[:], T.jf[:], A.mult)
+    ts(["x6"], ["pd"], T.pd[:], T.x6[:, 0:5], -65536.0, A.is_lt)
+    tp(["mmV"], ["xfV"], T.xf[:, 0:256], T.mm[:, 0:256])
+    tp(["mmS"], ["xfS"], T.xf[:, 256:640], T.mm[:, 256:640])
+    xf = ["xfV", "xfS"]
+    tt(["pd", "jf", "jf2"], ["jt0"], T.jt[:, 5:10], T.pd[:], T.jf[:], A.mult)
+    def count(e):
+        act(xf + ["nx6"], ["jk%d" % e, "sm%d" % e], T.jk[:, 640 * e:640 * e + 640], T.xf[:], AF.Sign, bias=T.nx6[:, e:e + 1], accum_out=T.sm[:, e:e + 1])
+    count(0)
+    act(xf + ["okg", "ps12"], ["kg"], T.kg[:], T.xf[:, 0:640].indirect(T.okg[:, 0:5]), scale=P(12))
+    count(1)
+    count(2)
     for k in (0, 1):
-        ts(["xf", "xf3", "x6"], ["cb%d" % k], T.cb[:, 640 * k:640 * k + 640], T.xf[:, 0:640], T.x6[:, 4 + k:5 + k], A.is_gt)
-    ts(["xf", "xf3", "okg", "ps12"], ["kg"], T.kg[:], T.xf[:, 0:656].indirect(T.okg[:, 0:6]), P(12), A.mult)
+        ts(xf + ["x6"], ["cb%d" % k], T.cb[:, 640 * k:640 * k + 640], T.xf[:], T.x6[:, 3 + k:4 + k], A.is_gt)
     for k in (0, 1):
         scan(["cb%d" % k, "rs160"], ["cbs%d" % k], T.cbs[:, 640 * k:640 * k + 640], T.rs160[:], T.cb[:, 640 * k:640 * k + 640], 0.0, A.mult, A.add)
     tt(["kg", "cst"], ["va2"], T.va2[:], T.kg[:], T.cst[:], A.add)
-    ts(["jt0"], ["jt"], T.jt[:, 0:6], T.jt[:, 6:12], 10000.0, A.subtract)
+    ts(["jt0"], ["jt"], T.jt[:, 0:5], T.jt[:, 5:10], 10000.0, A.subtract)
     for k in (0, 1):
-        E("v", V.tensor_reduce, ["cbs%d" % k], ["sm%d" % (4 + k)], T.sm[:, 4 + k:5 + k], T.cbs[:, 640 * k + 159:640 * k + 640:160], AxisListType.X, A.add)
-    tt(["sm%d" % e for e in range(6)] + ["jt"], ["pm"], T.pm[:], T.sm[:], T.jt[:, 0:6], A.max)
-    ts(["pm"], ["pu"], T.pu[:, 0:4], T.pm[:, 0:4], 639.0, A.add, 0.5, A.mult)
-    copy(["pm"], ["pu"], T.pu[:, 4:6], T.pm[:, 4:6], add=True)
-    E("v", V.tensor_copy, ["pu", "va2"], ["w2"], T.w2[:, 0:976].indirect(T.pu[:, 0:6]), T.va2[:])
+        E("v", V.tensor_reduce, ["cbs%d" % k], ["sm%d" % (3 + k)], T.sm[:, 3 + k:4 + k], T.cbs[:, 640 * k + 159:640 * k + 640:160], AxisListType.X, A.add)
+    tt(["sm%d" % e for e in range(5)] + ["jt"], ["pm"], T.pm[:], T.sm[:], T.jt[:, 0:5], A.max)
+    ts(["pm"], ["pu"], T.pu[:, 0:3], T.pm[:, 0:3], 639.0, A.add, 0.5, A.mult)
+    copy(["pm"], ["pu"], T.pu[:, 3:5], T.pm[:, 3:5], add=True)
+    E("v", V.tensor_copy, ["pu", "va2"], ["w2"], T.w2[:, 0:960].indirect(T.pu[:, 0:5]), T.va2[:])
     tp(["w2"], ["w2t"], T.w2t[:], T.w2[:, 0:512])
     def ok_rows():
         tp(["k2"], ["ro"], T.ro[:], T.k2[:])
         D("y", "dok", T.ok[0:1, :], T.ro[0:16, 0:32], ["ro"], ["ok"], "par")
-        D("y", "dok", T.ok[1:2, :], T.ro[0:16, 32:64], ["ro"], ["ok"], "par")
+        D("y", "dok", T.ok[1:2, :], T.ro[16:32, 0:32], ["ro"], ["ok"], "par")
     later += [lambda k=k: tt(["w2t"], ["t3k"], T.t3[:, 16 * k:16 * k + 16], T.w2t[:, k:512:32], T.w2t[:, 16 + k:512:32], A.add, add=True) for k in (1, 2)]
     later += [lambda a=a: copy(["t3k"], ["c6"], T.c6[:, 32 * a:32 * a + 32], T.t3[32 * a:32 * a + 32, 16:48], add=True) for a in range(4)]
     later += [
         lambda: tt(["c6"], ["a6"], T.a6[:], T.c6[:, 0:64], T.c6[:, 64:128], A.add),
         lambda: tt(["a6"], ["c6b"], T.c6[:, 0:32], T.a6[:, 0:32], T.a6[:, 32:64], A.add),
-        lambda: ts(["c6b"], ["k2"], T.k2[:, 0:16], T.c6[:, 0:16], -1.0, A.mult, 1.0, A.subtract),
-        lambda: ts(["c6b"], ["k2"], T.k2[:, 32:48], T.c6[:, 16:32], 1.0, A.subtract, add=True),
+        lambda: ts(["c6b"], ["k2"], T.k2[:], T.c6[:, 0:32], 1.0, A.subtract),
         ok_rows]
-    tt(["w2t"], ["t3"], T.t3[:, 0:16], T.w2t[:, 0:512:32], T.w2t[:, 16:512:32], A.add)
-    gap()
     for a in range(4):
-        copy(["t3"], ["c5"], T.c5[:, 16 * a:16 * a + 16], T.t3[32 * a:32 * a + 32, 0:16], add=True)
-    gap()
+        tt(["w2t"], ["c5"], T.c5[:, 16 * a:16 * a + 16], T.w2t[32 * a:32 * a + 32, 0:512:32], T.w2t[32 * a:32 * a + 32, 16:512:32], A.add, add=True)
+    gap(2)
     tt(["c5"], ["a5"], T.a5[:], T.c5[:, 0:32], T.c5[:, 32:64], A.add)
     gap()
-    tt(["a5"], ["sr"], T.sr[:, 0:16], T.a5[:, 0:16], T.a5[:, 16:32], A.add)
+    for a in range(4):
+        tt(["a5"], ["sr"], T.sr[32 * a:32 * a + 32, 0:16], T.a5[:, 0:16], T.a5[:, 16:32], A.add, add=a > 0)
     gap()
     tp(["sr"], ["sx"], T.sx[:], T.sr[:])
     gap()
@@ -356,9 +371,8 @@ def rank_program(g, core, T, topo):
     gap()
     tp(["sy"], ["so"], T.so[:], T.sy[:])
     gap()
-    for a in range(4):
-        copy(["so"], ["of2"], T.of2[32 * a:32 * a + 32, 0:32:2], T.so[:, 0:16], add=True)
-        copy(["so"], ["of2"], T.of2[32 * a:32 * a + 32, 1:32:2], T.so[:, 32:48], add=True)
+    copy(["so"], ["of2"], T.of2[:, 0:32:2], T.so[:, 0:16])
+    copy(["so"], ["of2"], T.of2[:, 1:32:2], T.so[:, 32:48], add=True)
     wr["lca"], wr["lsa"] = [("rc", None)], [("rs", None)]
     land, lands = ["lca", "lco", "lcz"], ["lsa", "lso", "lsz"]
     for k in (0, 1):
@@ -377,8 +391,10 @@ def rank_program(g, core, T, topo):
     act(lands + ["of2"], ["fz"], T.fz[:], T.ls[:, 0:656].indirect(T.of2[:, 0:32]))
     for k in range(4):
         D("s", "dos", T.osc[4 * k:4 * k + 4, :], T.fz[32 * k:32 * k + 4, :], ["fz"], ["osc"], "par")
-    copy(ys, ["yo1"], T.yo[:, 256:512], T.yf[:, 0:656].indirect(T.of2[:, 16:32]))
-    D("y", "dy2", T.y[:, 256:512], T.yo[:, 256:512], ["yo1"], ["y"], "par")
+    for k in (0, 1):
+        c = 256 + 128 * k
+        copy(ys, ["yo%d" % (1 + k)], T.yo[:, c:c + 128], T.yf[:, 0:656].indirect(T.of2[:, 16 + 8 * k:24 + 8 * k]))
+        D("y", ["dy2", "dy3"][k], T.y[:, c:c + 128], T.yo[:, c:c + 128], ["yo%d" % (1 + k)], ["y"], "par")
     gap(len(later))
     for n in SEMAPHORES:
         if tot[n]:

from concourse.bass import DstId, RemoteDMATransfer
from concourse.mybir import dt, AluOpType, AxisListType, ActivationFunctionType

SCRATCH = {"mykd": ("dram", [128, 8], "int32"), "kd0": ("dram", [4, 128, 8], "int32"), "kd1": ("dram", [4, 128, 8], "int32"),
           "acc": ("psum", [128, 1024], "float32")}
SIZES = {
    (128, "float32"): "tkf:32 blo:32 m0:512 xb:512 xg:256 val:256 vk:256 vc:256 vd:256 ta0:32 ta1:32 bl0:32 bl1:32 ps:32 it:1040 ix:112 im:80 mh:40 ico:160 irk:240 "
                      "cst:80 jf:5 pd:5 jt:10 s0:16 wi:1040 wt:768 qk:24 qi:32 xt:32 yy:64 ot:64 kx:24 mm:640 xf:640 x6:16 nx6:16 sm:5 "
                      "pm:5 kg:80 va2:80 w2:960 w2t:512 t3:48 sr:32 sx:32 sy:64 so:64 yf:656 yo:512",
    (32, "float32"): "tr:16 spf:1 spm:32 spb:32 d7:112 d7s:112 rs7:112 d96:20 c4:64 a2:32 kb:20 f1:16 nk:16 zz:20 pl:64 pt:64 cc:64 cy:32 "
                     "pq:16 pf:16 c5:64 a5:32 c6:128 a6:64 k2:32 ro:32",
    (128, "bfloat16"): "cm0:512 cm1:512 ct0:512 ct1:512 cs0:512 cs1:512 eq:512 et:512 es:512 rs32:512 rs16:512 rs160:640 zb:512 wb:512 jk:1920 cb:1280 cbs:1280",
    (128, "int32"): "tk:32 ti0:32 ti1:32 pi:8", (32, "int32"): "spi:1",
    (128, "uint16"): "xu:512 of0:16 of1:16 mb:32 mo:40 oxn:32 oxg:16 ovk:16 okg:6 ox6:2 pw:16 off:48 pu:6 of2:32",
    (128, "float8_e4m3fn_x4"): "zc:128 kcs:512 qc:640 lc:656 fc:512 wc:128",
    (128, "uint8"): "zs:128 kss:512 qs:640 ls:672 fz:512 wz:128"}
for (_p, _d), _l in SIZES.items():
    for _x in _l.split():
        SCRATCH[_x.split(":")[0]] = ("sbuf", [_p, int(_x.split(":")[1])], _d)
SEMAPHORES = ["vs", "ss", "ts", "gs", "dk", "dt", "dsp", "dw", "dkc", "dz", "dta", "dtb", "dkx", "doc", "doc2", "dos", "dy", "dy2", "dy3", "dok",
              "rk", "rx", "rc", "rs", "loc"]


def rank_program(g, core, T, topo):
    s = T.rank_of(core)
    if s is None:
        return
    A, N = AluOpType, len(T.cores)
    AF = ActivationFunctionType
    q_of = {"v": g.vector, "s": g.scalar, "t": g.tensor, "g": g, "y": g.sync}
    own = {"v": "vs", "s": "ss", "t": "ts", "g": "gs"}
    tot = {n: 0 for n in SEMAPHORES}
    seen = {q: {} for q in q_of}
    wr, rd = {}, {}

    def need(q, r, w, add=False):
        deps = [(d, 0) for t in r for d in wr.get(t, [])]
        deps += [(d, 1) for t in w for d in wr.get(t, []) + rd.get(t, [])]
        for (sem, n), order in deps:
            if order and add and own.get(q) == sem:
                continue
            n = tot[sem] if n is None else n
            if seen[q].get(sem, 0) < n:
                q_of[q].wait_ge(T.sem[sem], n)
                seen[q][sem] = n

    def note(me, r, w, add=False):
        for t in r:
            rd.setdefault(t, []).append(me)
        for t in w:
            wr[t] = wr.get(t, []) + [me] if add else [me]
            if not add:
                rd[t] = []

    def E(q, call, r, w, *args, add=False, **kw):
        need(q, r, w, add)
        sem = own[q]
        call(*args, **kw).then_inc(T.sem[sem], 1)
        tot[sem] += 1
        note((sem, tot[sem]), r, w, add)

    def D(q, sem, out, in_, r, w, add=True):
        need(q, r, [] if add == "par" else w)
        q_of[q].dma_start(out, in_).then_inc(T.sem[sem], 16)
        tot[sem] += 16
        note((sem, None), r, w, True)

    V, S = g.vector, g.scalar

    def copy(r, w, out, in_, add=False): E("v", V.tensor_copy, r, w, out, in_, add=add)
    def tt(r, w, out, a, b, op, add=False): E("v", V.tensor_tensor, r, w, out, a, b, op, add=add)
    def ts(r, w, out, a, s1, op, s2=None, op1=None, add=False):
        if op1 is None: E("v", V.tensor_scalar, r, w, out, a, s1, None, op, add=add)
        else: E("v", V.tensor_scalar, r, w, out, a, s1, s2, op, op1, add=add)
    def tp(r, w, out, in_, add=False): E("v", V.transpose, r, w, out, in_, add=add)
    def scan(r, w, out, a, b, init, o0, o1, add=False): E("v", V.tensor_tensor_scan, r, w, out, a, b, init, o0, o1, add=add)
    def fill(w, ap, c, add=False): E("v", V.memset, [], w, ap, c, add=add)
    def act(r, w, out, in_, fn=AF.Copy, **kw): E("s", S.activation, r, w, out, in_, fn, **kw)
    def iota(w, ap, pat, base, mult=0):
        E("g", g.iota, [], w, ap, pat, base, mult, allow_small_or_imprecise_dtypes=True)

    later = []

    def gap(n=1):
        for _ in range(min(n, len(later))):
            later.pop(0)()

    def fused(pairs, sem, per, r):
        need("g", r, [])
        tr = []
        for i, (c, dst, src) in enumerate(pairs):
            rid, pid, _ = topo.addr(c)
            e = topo.engines(core, c)[per * i:per * (i + 1)]
            tr.append(RemoteDMATransfer(dst_ids=[DstId(rid=rid, pnc=pid)], dma_engine_mask=sum(1 << k for k in e),
                                        remote_sem=T.sem[sem], src=src, dst=dst))
        g.remote_dma_fused(tr, local_sem=T.sem.loc)
        tot["loc"] += per * len(pairs)

    passes = [h for h in (0, 1) if any(2 * a + h > s for a in range(4))]
    first = {h: min(a for a in range(4) if 2 * a + h > s) for h in passes}
    odd = s % 2

    if s > 0:
        for k in (0, 1):
            D("y" if k == 0 else "s", "dk", T.mykd[64 * k:64 * k + 64, :], T.ky[:], [], ["mykd"], "par")
    for k in range(8):
        D("y" if k % 2 == 0 else "s", "dt", T.tk[16 * k:16 * k + 16, :], T.ky[:], [], ["tk"], "par")
    for k in (0, 1):
        D("y", "dsp", T.spi[16 * k:16 * k + 16, :], T.sp[:], [], ["spi"], "par")
    D("y", "dkc", T.kcs[:].bitcast(dt.uint8), T.kc[:], [], ["kcs"], "par")
    D("y", "dkc", T.kss[:], T.ks[:], [], ["kss"], "par")
    D("y", "dw", T.wb[:], T.w[:], [], ["wb"], "par")

    iota(["pi"], T.pi[:, 0:1], [[0, 1]], 0, 1)
    iota(["imb"], T.ix[:, 0:32], [[1, 16], [0, 2]], 0)
    iota(["ixn"], T.ix[:, 48:80], [[64, 8], [16, 2], [32, 2]], 0)
    iota(["ixg"], T.ix[:, 80:96], [[64, 8], [16, 2]], 0)
    iota(["ivk"], T.ix[:, 96:112], [[32, 16]], 0)
    if s > 0:
        fused([(T.cores[r], T["kd%d" % odd][s // 2], T.mykd[:]) for r in range(s)], "rk", 1, ["mykd"])
    iota(["vc"], T.vc[:], [[1, 16], [16, 16]], 0)
    iota(["d96"], T.d96[:], [[0, 20]], 0)
    if not passes:
        iota(["kb"], T.kb[:], [[0, 20]], 1)
    iota(["kb"], T.kb[:, 0:1], [[0, 1]], 0)
    iota(["im2"], T.im[:, 40:80], [[0, 4], [1, 5], [0, 2]], 0)
    iota(["im"], T.im[:, 0:40], [[6, 4], [1, 5], [0, 2]], 0)
    iota(["tr"], T.tr[:], [[16, 16]], 768, 1)
    for n, c in (("zz", 20), ("pl", 64), ("cc", 64), ("qi", 32)):
        iota([n], T[n][:], [[0, c]], 0)
    iota(["ikg"], T.ix[:, 32:37], [[32, 5]], 0)
    iota(["irk"], T.irk[:, 0:80], [[1, 5], [0, 16]], 0)
    iota(["it"], T.it[:], [[-1, 1040]], -(66000 + 768 * s))
    iota(["ico"], T.ico[:, 0:80], [[32, 5], [1, 16]], 16)
    iota(["jf"], T.jf[:, 0:3], [[32, 3]], 10897, 2)
    iota(["jf2"], T.jf[:, 3:5], [[16, 2]], 10816, 1)
    for n, c in (("sr", 32), ("k2", 32)):
        iota([n], T[n][:], [[0, c]], 0)

    for h in passes:
        if first[h]:
            fill(["ti%d" % h], T["ti%d" % h][0:32 * first[h], :], -1)
    ts(["pi"], ["pi1"], T.pi[:, 1:2], T.pi[:, 0:1], 15, A.bitwise_and)
    ts(["pi"], ["pi2"], T.pi[:, 2:3], T.pi[:, 0:1], 4, A.logical_shift_right, 1, A.bitwise_and)
    ts(["pi"], ["pi3"], T.pi[:, 3:4], T.pi[:, 0:1], 5, A.logical_shift_right)
    fill(["rs32"], T.rs32[:], 1.0)
    fill(["rs7"], T.rs7[:], 1.0)
    copy(["pi1", "pi2", "pi3"], ["ps"], T.ps[:, 0:3], T.pi[:, 1:4])
    P = lambda k: T.ps[:, k:k + 1]
    copy(["imb"], ["mb"], T.mb[:], T.ix[:, 0:32])
    fill(["rs16"], T.rs16[:], 1.0)
    ts(["ps"], ["ps3"], P(3), P(1), 16.0, A.mult, P(0), A.add)
    ts(["ps"], ["ps4"], P(4), P(1), 32.0, A.mult, P(0), A.add)
    ts(["ps"], ["ps7"], P(7), P(1), 256.0, A.mult)
    ts(["ps"], ["ps10"], P(10), P(0), 0.0, A.is_equal)
    ts(["ps"], ["ps11"], P(11), P(0), 0.0, A.not_equal, -1.0, A.mult)
    ts(["ps"], ["ps14"], P(14), P(0), 0.0, A.not_equal)
    ts(["ixn", "ps"], ["oxn"], T.oxn[:], T.ix[:, 48:80], P(0), A.add)
    ts(["ixg", "ps4"], ["oxg"], T.oxg[:], T.ix[:, 80:96], P(4), A.add)
    ts(["ivk", "ps3"], ["ovk"], T.ovk[:], T.ix[:, 96:112], P(3), A.add)
    ts(["ps7", "ps10"], ["ps16"], P(16), P(7), P(10), A.mult)
    fill(["rs7"], T.rs7[:, 0:112:7], 0.0)
    fill(["rs32"], T.rs32[:, 0:512:32], 0.0)
    fill(["rs16"], T.rs16[:, 0:512:16], 0.0)
    copy(["tk"], ["tkf"], T.tkf[:], T.tk[:])
    copy(["spi"], ["spf"], T.spf[:], T.spi[:])
    tp(["tkf"], ["blo"], T.blo[:], T.tkf[:])
    ts(["tkf", "spf"], ["spm"], T.spm[:], T.tkf[0:32, :], 0.0, A.mult, T.spf[:, 0:1], A.add)
    copy(["blo", "mb"], ["m0"], T.m0[:], T.blo[:, 0:32].indirect(T.mb[:, 0:32]))
    tp(["spm"], ["spb"], T.spb[:], T.spm[:])
    tp(["m0"], ["xb"], T.xb[:], T.m0[:])
    if passes:
        act(["xb", "oxg"], ["xg"], T.xg[:], T.xb[:, 0:512].indirect(T.oxg[:, 0:16]))
    act(["xb", "ovk", "ps11"], ["vk"], T.vk[:], T.xb[:, 0:512].indirect(T.ovk[:, 0:16]), scale=P(11))
    act(["vc", "ps10", "ps16"], ["vd"], T.vd[:], T.vc[:], AF.Identity, scale=P(10), bias=P(16))
    act(["it", "ps14"], ["wi"], T.wi[:], T.it[:], scale=P(14))
    act(["it"], ["w2"], T.w2[:], T.it[:, 0:960], scale=0.0)
    act(["it"], ["yfz"], T.yf[:, 0:16], T.it[:, 0:16], scale=0.0)
    for e in range(N - 1):
        ts(["blo", "spb"], ["d7"], T.d7[:, e:112:7], T.blo[0:32, 0:16], T.spb[:, e:e + 1], A.is_ge, 96.0, A.mult, add=True)
    if passes:
        copy(["xb", "oxn"], ["xu"], T.xu[:], T.xb[:, 0:512].indirect(T.oxn[:, 0:32]))
    scan(["d7", "rs7"], ["d7s"], T.d7s[:], T.rs7[:], T.d7[:], 0.0, A.mult, A.add)
    tt(["vk", "vd"], ["val"], T.val[:], T.vk[:], T.vd[:], A.add)
    ts(["d7s"], ["d96"], T.d96[:, 0:16], T.d7s[:, 6:112:7], 16.0 * odd, A.add)
    fill(["rs160"], T.rs160[:], 1.0)

    later += [
        lambda: ts(["im2", "ps"], ["mh"], T.mh[:], T.im[:, 40:80], P(1), A.add, 3.0, A.is_ge),
        lambda: ts(["ps"], ["ps18"], P(18), P(0), P(1), A.add, 3.0, A.is_ge),
        lambda: ts(["ps"], ["ps9"], P(9), P(2), 6.0, A.mult, P(0), A.add),
        lambda: ts(["ps"], ["ps6"], P(6), P(1), 16.0, A.mult),
        lambda: tt(["im", "mh"], ["mo"], T.mo[:], T.im[:, 0:40], T.mh[:], A.add),
        lambda: ts(["ps", "ps3"], ["ps5"], P(5), P(2), 160.0, A.mult, P(3), A.add),
        lambda: ts(["ps9", "ps18"], ["ps19"], P(19), P(9), P(18), A.add),
        lambda: ts(["ps", "ps6"], ["ps15"], P(15), P(2), 160.0, A.mult, P(6), A.add),
        lambda: ts(["ps"], ["ps8"], P(8), P(2), 2.0, A.mult, 1.0, A.add),
        lambda: ts(["ps19"], ["ox6"], T.ox6[:, 0:1], P(19), 23.0, A.min),
        lambda: ts(["ps"], ["ps13"], P(13), P(0), 2.0, A.is_equal),
        lambda: ts(["ps"], ["ps12"], P(12), P(0), 1.0, A.is_equal, -1.0, A.mult),
        lambda: ts(["ps15", "ps10"], ["ps17"], P(17), P(15), P(10), A.mult),
        lambda: ts(["ikg", "ps5"], ["okg"], T.okg[:, 0:5], T.ix[:, 32:37], P(5), A.add),
        lambda: ts(["irk", "ps"], ["irk1"], T.irk[:, 80:160], T.irk[:, 0:80], P(1), A.add, 3.0, A.is_ge),
        lambda: ts(["ps8", "ps13", "ps12"], ["ps20"], P(20), P(8), P(13), A.mult, P(12), A.subtract),
        lambda: fill(["rs160"], T.rs160[:, 0:640:160], 0.0)]

    if passes:
        tot["rk"] = N - 1 - s
        wr["rk"] = [("rk", None)]
        for h in passes:
            a = first[h]
            D("y", "dta" if h == 0 else "dtb", T["ti%d" % h][32 * a:128, :], T["kd%d" % h][a:4], ["rk"], ["ti%d" % h], True)
        H = ["%d" % h for h in passes]
        for h in H: copy(["ti" + h], ["ta" + h], T["ta" + h][:], T["ti" + h][:])
        for h in H: tp(["ta" + h], ["bl" + h], T["bl" + h][:], T["ta" + h][:])
        for h in H: ts(["xu", "bl" + h], ["cm" + h], T["cm" + h][:], T.xu[:], T["bl" + h][:, 0:1], A.is_ge)
        for h in H: tp(["cm" + h], ["ct" + h], T["ct" + h][:], T["cm" + h][:])
        for h in H: scan(["ct" + h, "rs32"], ["cs" + h], T["cs" + h][:], T.rs32[:], T["ct" + h][:], 0.0, A.mult, A.add)
        for h in H: ts(["cs" + h], ["of" + h], T["of" + h][:], T["cs" + h][:, 31:512:32], 1.0, A.subtract, 0.0, A.max)
        for i, h in enumerate(H):
            tt(["ta" + h, "of" + h, "xg"], ["eq"], T.eq[:, 256 * i:256 * i + 256], T["ta" + h][:, 0:32].indirect(T["of" + h][:, 0:16]), T.xg[:], A.is_equal, add=True)
        n = 256 * len(H)
        tp(["eq"], ["et"], T.et[:, 0:n], T.eq[:, 0:n])
        gap()
        scan(["et", "rs16"], ["es"], T.es[:, 0:n], T.rs16[:, 0:n], T.et[:, 0:n], 0.0, A.mult, A.add)
        gap()
        if len(H) == 2: tt(["es"], ["s0"], T.s0[:], T.es[:, 15:256:16], T.es[:, 271:512:16], A.add)
        else: copy(["es"], ["s0"], T.s0[:], T.es[:, 15:256:16])
        gap()
        quads = list(range(min(first.values()), 4))
        nq = len(quads)
        C4 = lambda i: T.c4[:, 16 * i:16 * i + 16]
        for i, a in enumerate(quads):
            at = [0, 2, 1, 3][i] if nq == 4 else i
            if i < (nq + 1) // 2: copy(["s0"], ["c4"], C4(at), T.s0[32 * a:32 * a + 32, :], add=True)
            else: ts(["s0"], ["c4"], C4(at), T.s0[32 * a:32 * a + 32, :], -1.0, A.mult, add=True)
        gap()
        if nq == 4:
            tt(["c4"], ["a2"], T.a2[:], T.c4[:, 0:32], T.c4[:, 32:64], A.add)
            gap()
            x, y, r = T.a2[:, 0:16], T.a2[:, 16:32], ["a2"]
        elif nq == 3:
            tt(["c4"], ["a2"], T.a2[:, 0:16], C4(0), C4(1), A.add)
            gap()
            x, y, r = T.a2[:, 0:16], C4(2), ["a2", "c4"]
        else:
            x, y, r = C4(0), C4(1), ["c4"]
        if nq == 1:
            ts(r, ["kb"], T.kb[:, 1:17], x, 0.0, A.is_equal)
            ts(r, ["f1"], T.f1[:], x, 0.0, A.is_gt)
        else:
            tt(r, ["kb"], T.kb[:, 1:17], x, y, A.is_equal)
            tt(r, ["f1"], T.f1[:], x, y, A.not_equal)
    scan(["kb", "zz"], ["pl"], T.pl[:, 0:17], T.kb[:, 0:17], T.zz[:, 0:17], 0.0, A.add, A.add)
    scan(["kb", "d96"], ["pl"], T.pl[:, 32:49], T.kb[:, 0:17], T.d96[:, 0:17], 0.0, A.add, A.max, add=True)
    gap()
    tp(["pl"], ["pt"], T.pt[:], T.pl[:])
    if passes: tt(["f1", "tr"], ["nk"], T.nk[:], T.f1[:], T.tr[:], A.mult)
    scan(["pt"], ["cc"], T.cc[:, 1:33], T.pt[:, 0:32], T.pt[:, 32:64], 0.0, A.add, A.max)
    gap()
    tp(["cc"], ["cy"], T.cy[:], T.cc[:, 0:32])
    gap()
    scan(["kb", "d96", "cy"], ["pq"], T.pq[:], T.kb[:, 0:16], T.d96[:, 0:16], T.cy[:, 16:17], A.add, A.max)
    src, tok = T.pq, "pq"
    gap()
    if passes:
        tt(["pq", "nk"], ["pf"], T.pf[:], T.pq[:], T.nk[:], A.max)
        src, tok = T.pf, "pf"
        gap()
    for a in range(4):
        copy([tok], ["pw"], T.pw[32 * a:32 * a + 32, :], src[:], add=True)
    gap()
    E("v", V.tensor_copy, ["pw", "val"], ["wi"], T.wi[:, 0:1040].indirect(T.pw[:, 0:16]), T.val[:])
    gap()
    tp(["wi"], ["wt"], T.wt[:], T.wi[:, 0:768])
    gap()
    tt(["wt"], ["qk"], T.qk[:], T.wt[:, 1:768:32], T.wt[:, 17:768:32], A.max)
    tt(["wt"], ["qi"], T.qi[:, 0:24], T.wt[:, 0:768:32], T.wt[:, 16:768:32], A.max)
    peers = [(s + i) % N for i in range(1, N)]
    fused([(T.cores[d], T.kx[:, 3 * s:3 * s + 3], T.qk[:, 3 * d:3 * d + 3]) for d in peers], "rx", 2, ["qk"])
    D("y", "dkx", T.kx[:, 3 * s:3 * s + 3], T.qk[:, 3 * s:3 * s + 3], ["qk"], ["kx"], "par")
    gap()
    tp(["qi"], ["xt"], T.xt[:], T.qi[:])
    gap()
    for k in range(4):
        copy(["xt"], ["yy"], T.yy[:, 16 * k:16 * k + 16], T.xt[:, 16 * (k // 2):16 * (k // 2) + 16], add=True)
    gap()
    tp(["yy"], ["ot"], T.ot[:], T.yy[:])
    gap()
    if odd:
        copy(["ot"], ["off"], T.off[:, 0:48:2], T.ot[:, 32:56])
        copy(["ot"], ["off"], T.off[:, 1:47:2], T.ot[:, 1:24], add=True)
    else:
        copy(["ot"], ["off"], T.off[:, 0:48:2], T.ot[:, 0:24])
        copy(["ot"], ["off"], T.off[:, 1:48:2], T.ot[:, 32:56], add=True)
    def pick(d, cbuf, sbuf, c, tc, tz):
        E("v", V.tensor_copy, ["off", "kcs"], [tc], cbuf[:, c:c + 80].bitcast(dt.uint32), T.kcs[:, 0:512].bitcast(dt.uint32).indirect(T.off[:, 6 * d:6 * d + 5]))
        act(["off", "kss"], [tz], sbuf[:, c:c + 80], T.kss[:, 0:512].indirect(T.off[:, 6 * d:6 * d + 5]))
    for d in peers: pick(d, T.qc, T.qs, 80 * d, "qc%d" % d, "qs%d" % d)
    pick(s, T.lc, T.ls, 16 + 80 * s, "lco", "lso")
    me = 16 + 80 * s
    for part in (peers[:1], peers[1:3], peers[3:]):
        e = len(topo.engines(core, T.cores[part[0]])) // len(part)
        fused([(T.cores[d], T.lc[:, me:me + 80].bitcast(dt.uint8), T.qc[:, 80 * d:80 * d + 80].bitcast(dt.uint8)) for d in part], "rc", e, ["qc%d" % d for d in part])
        fused([(T.cores[d], T.ls[:, me:me + 80], T.qs[:, 80 * d:80 * d + 80]) for d in part], "rs", e, ["qs%d" % d for d in part])
        for r in part:
            tot["rc"] += e
            tot["rs"] += e
    gap(len(later))
    act(["ico", "ps17", "ps10"], ["ico2"], T.ico[:, 80:160], T.ico[:, 0:80], AF.Identity, scale=P(10), bias=P(17))
    act(["irk1", "ps20", "ps13"], ["irk2"], T.irk[:, 160:240], T.irk[:, 80:160], AF.Identity, scale=P(13), bias=P(20))
    E("v", V.quantize_mx, ["wb"], ["wc", "wz"], T.wc[:], T.wz[:], T.wb[:])
    fill(["zb"], T.zb[:], 0.0)
    tt(["ico2", "irk2"], ["cst"], T.cst[:], T.ico[:, 80:160], T.irk[:, 160:240], A.add)
    E("v", V.quantize_mx, ["zb"], ["zc", "zs"], T.zc[:], T.zs[:], T.zb[:])
    D("y", "dz", T.lc[:, 0:1].bitcast(dt.uint8), T.zc[:, 0:1].bitcast(dt.uint8), ["zc"], ["lcz"], "par")
    D("y", "dz", T.ls[:, 0:1], T.zs[:, 0:1], ["zs"], ["lsz"], "par")
    tot["rx"] = 2 * (N - 1)
    wr["rx"] = [("rx", None)]
    act(["rx", "kx", "mo"], ["mmS"], T.mm[:, 256:640], T.kx[:, 0:24].indirect(T.mo[:, 16:40]))
    copy(["rx", "kx", "ox6"], ["x6"], T.x6[:], T.kx[:, 0:24].indirect(T.ox6[:, 0:1]))
    copy(["rx", "kx", "mo"], ["mmV"], T.mm[:, 0:256], T.kx[:, 0:24].indirect(T.mo[:, 0:16]))
    ts(["x6"], ["nx6"], T.nx6[:], T.x6[:], -1.0, A.mult)
    ts(["x6"], ["pd"], T.pd[:], T.x6[:, 0:5], -65536.0, A.is_lt)
    tp(["mmV"], ["xfV"], T.xf[:, 0:256], T.mm[:, 0:256])
    tp(["mmS"], ["xfS"], T.xf[:, 256:640], T.mm[:, 256:640])
    xf = ["xfV", "xfS"]
    tt(["pd", "jf", "jf2"], ["jt0"], T.jt[:, 5:10], T.pd[:], T.jf[:], A.mult)
    def count(e):
        act(xf + ["nx6"], ["jk%d" % e, "sm%d" % e], T.jk[:, 640 * e:640 * e + 640], T.xf[:], AF.Sign, bias=T.nx6[:, e:e + 1], accum_out=T.sm[:, e:e + 1])
    count(0)
    act(xf + ["okg", "ps12"], ["kg"], T.kg[:], T.xf[:, 0:640].indirect(T.okg[:, 0:5]), scale=P(12))
    count(1)
    count(2)
    for k in (0, 1):
        ts(xf + ["x6"], ["cb%d" % k], T.cb[:, 640 * k:640 * k + 640], T.xf[:], T.x6[:, 3 + k:4 + k], A.is_gt)
    for k in (0, 1):
        scan(["cb%d" % k, "rs160"], ["cbs%d" % k], T.cbs[:, 640 * k:640 * k + 640], T.rs160[:], T.cb[:, 640 * k:640 * k + 640], 0.0, A.mult, A.add)
    tt(["kg", "cst"], ["va2"], T.va2[:], T.kg[:], T.cst[:], A.add)
    ts(["jt0"], ["jt"], T.jt[:, 0:5], T.jt[:, 5:10], 10000.0, A.subtract)
    for k in (0, 1):
        E("v", V.tensor_reduce, ["cbs%d" % k], ["sm%d" % (3 + k)], T.sm[:, 3 + k:4 + k], T.cbs[:, 640 * k + 159:640 * k + 640:160], AxisListType.X, A.add)
    tt(["sm%d" % e for e in range(5)] + ["jt"], ["pm"], T.pm[:], T.sm[:], T.jt[:, 0:5], A.max)
    ts(["pm"], ["pu"], T.pu[:, 0:3], T.pm[:, 0:3], 639.0, A.add, 0.5, A.mult)
    copy(["pm"], ["pu"], T.pu[:, 3:5], T.pm[:, 3:5], add=True)
    E("v", V.tensor_copy, ["pu", "va2"], ["w2"], T.w2[:, 0:960].indirect(T.pu[:, 0:5]), T.va2[:])
    tp(["w2"], ["w2t"], T.w2t[:], T.w2[:, 0:512])
    def ok_rows():
        tp(["k2"], ["ro"], T.ro[:], T.k2[:])
        D("y", "dok", T.ok[0:1, :], T.ro[0:16, 0:32], ["ro"], ["ok"], "par")
        D("y", "dok", T.ok[1:2, :], T.ro[16:32, 0:32], ["ro"], ["ok"], "par")
    later += [lambda k=k: tt(["w2t"], ["t3k"], T.t3[:, 16 * k:16 * k + 16], T.w2t[:, k:512:32], T.w2t[:, 16 + k:512:32], A.add, add=True) for k in (1, 2)]
    later += [lambda a=a: copy(["t3k"], ["c6"], T.c6[:, 32 * a:32 * a + 32], T.t3[32 * a:32 * a + 32, 16:48], add=True) for a in range(4)]
    later += [
        lambda: tt(["c6"], ["a6"], T.a6[:], T.c6[:, 0:64], T.c6[:, 64:128], A.add),
        lambda: tt(["a6"], ["c6b"], T.c6[:, 0:32], T.a6[:, 0:32], T.a6[:, 32:64], A.add),
        lambda: ts(["c6b"], ["k2"], T.k2[:], T.c6[:, 0:32], 1.0, A.subtract),
        ok_rows]
    for a in range(4):
        tt(["w2t"], ["c5"], T.c5[:, 16 * a:16 * a + 16], T.w2t[32 * a:32 * a + 32, 0:512:32], T.w2t[32 * a:32 * a + 32, 16:512:32], A.add, add=True)
    gap(2)
    tt(["c5"], ["a5"], T.a5[:], T.c5[:, 0:32], T.c5[:, 32:64], A.add)
    gap()
    for a in range(4):
        tt(["a5"], ["sr"], T.sr[32 * a:32 * a + 32, 0:16], T.a5[:, 0:16], T.a5[:, 16:32], A.add, add=a > 0)
    gap()
    tp(["sr"], ["sx"], T.sx[:], T.sr[:])
    gap()
    for k in range(4):
        copy(["sx"], ["sy"], T.sy[:, 16 * k:16 * k + 16], T.sx[:, 16 * (k // 2):16 * (k // 2) + 16], add=True)
    gap()
    tp(["sy"], ["so"], T.so[:], T.sy[:])
    gap()
    copy(["so"], ["of2"], T.of2[:, 0:32:2], T.so[:, 0:16])
    copy(["so"], ["of2"], T.of2[:, 1:32:2], T.so[:, 32:48], add=True)
    wr["lca"], wr["lsa"] = [("rc", None)], [("rs", None)]
    land, lands = ["lca", "lco", "lcz"], ["lsa", "lso", "lsz"]
    for k in (0, 1):
        c = 16 + 320 * k
        E("t", g.tensor.matmul_mx, land + lands + ["wc", "wz"], ["acc%d" % k], T.acc[:, 512 * k:512 * k + 320], T.wc[:], T.wz[:], T.lc[:, c:c + 320], T.ls[:, c:c + 320], True, True)
    for k in (0, 1):
        act(["acc%d" % k], ["yf%d" % k], T.yf[:, 16 + 320 * k:336 + 320 * k], T.acc[:, 512 * k:512 * k + 320])
    ys = ["yfz", "yf0", "yf1", "of2"]
    def codes(k):
        E("v", V.tensor_copy, land + ["of2"], ["fc%d" % k], T.fc[:, 256 * k:256 * k + 256].bitcast(dt.uint32), T.lc[:, 0:656].bitcast(dt.uint32).indirect(T.of2[:, 16 * k:16 * k + 16]))
        D("y", ["doc", "doc2"][k], T.oc[:, 1024 * k:1024 * k + 1024], T.fc[:, 256 * k:256 * k + 256].bitcast(dt.uint8), ["fc%d" % k], ["oc"], "par")
    codes(0)
    act(ys, ["yo0"], T.yo[:, 0:256], T.yf[:, 0:656].indirect(T.of2[:, 0:16]))
    D("y", "dy", T.y[:, 0:256], T.yo[:, 0:256], ["yo0"], ["y"], "par")
    codes(1)
    act(lands + ["of2"], ["fz"], T.fz[:], T.ls[:, 0:656].indirect(T.of2[:, 0:32]))
    for k in range(4):
        D("s", "dos", T.osc[4 * k:4 * k + 4, :], T.fz[32 * k:32 * k + 4, :], ["fz"], ["osc"], "par")
    for k in (0, 1):
        c = 256 + 128 * k
        copy(ys, ["yo%d" % (1 + k)], T.yo[:, c:c + 128], T.yf[:, 0:656].indirect(T.of2[:, 16 + 8 * k:24 + 8 * k]))
        D("y", ["dy2", "dy3"][k], T.y[:, c:c + 128], T.yo[:, c:c + 128], ["yo%d" % (1 + k)], ["y"], "par")
    gap(len(later))
    for n in SEMAPHORES:
        if tot[n]:
            g.wait_ge(T.sem[n], tot[n])
